import numpy as np
import ml_dtypes


def mxq(x, axis, fmt="e4m3"):
    dtype, down = {"e4m3": (ml_dtypes.float8_e4m3fn, 7), "e5m2": (ml_dtypes.float8_e5m2, 14)}[fmt]
    v = np.moveaxis(np.asarray(x, np.float32).astype(ml_dtypes.bfloat16).astype(np.float64), axis, -1)
    blocks = v.reshape(v.shape[:-1] + (-1, 32))
    amax = np.abs(blocks).max(-1, keepdims=True)
    byte = np.maximum(np.where(amax > 0, np.frexp(amax)[1] - 1 + 127, 0) - down, 1)
    scale = np.exp2(byte - 127.0)
    codes = (blocks / scale).astype(np.float32).astype(dtype).astype(np.float64)
    return np.moveaxis((codes * scale).reshape(v.shape), -1, axis)


WIDE = False


def mx_kscale(k):
    if not WIDE:
        return np.ones(k)
    levels = np.array([10, -10, 5, -5, 0])
    if k % 512:
        return np.exp2(np.random.permutation(np.resize(levels, k // 32))).repeat(32)
    a = np.empty((k // 512, 16))
    for p in range(k // 512):
        a[p, :8] = np.random.permutation(np.resize(levels, 8))
        for g in range(8):
            far = levels[np.abs(levels - a[p, g]) >= 10]
            a[p, g + 8] = far[np.random.randint(len(far))]
    return np.exp2(a.ravel()).repeat(32)


def f64(x):
    return np.asarray(x).astype(np.float64)


def striped(idx):
    return np.tile(idx.reshape(-1, 16).T, (8, 1)).astype(np.uint16)


def unstriped(offs):
    return offs[:16].T.reshape(-1).astype(np.int64)


E2M1 = np.array([0.0, 0.5, 1.0, 1.5, 2.0, 3.0, 4.0, 6.0, -0.0, -0.5, -1.0, -1.5, -2.0, -3.0, -4.0, -6.0])


def pack_weight(w, fmt):
    k, n = w.shape
    w = f64(np.asarray(w, np.float32).astype(ml_dtypes.bfloat16)).reshape(k // 32, 32, n)
    amax = np.abs(w).max(1)
    if fmt == "e4m3":
        byte = np.frexp(amax)[1] - 1 + 127 - 7
    else:
        mant, ex = np.frexp(amax / 6.0)
        byte = np.where(mant > 0.5, ex, ex - 1) + 127
    byte = np.clip(np.where(amax > 0, byte, 1), 1, 254)
    scaled = (w * np.exp2(127.0 - byte)[:, None, :]).reshape(k, n).astype(np.float32)
    by_word = np.ascontiguousarray(scaled.reshape(k // 512, 128, 4, n).transpose(0, 1, 3, 2))
    if fmt == "e4m3":
        words = by_word.astype(ml_dtypes.float8_e4m3fn).view(np.uint8)
    else:
        c = by_word.astype(ml_dtypes.float4_e2m1fn).view(np.uint8) & 0xF
        words = (c[..., 0::2] | (c[..., 1::2] << 4)).reshape(k // 512, 128, 2 * n)
    return np.ascontiguousarray(words), np.ascontiguousarray(byte.astype(np.uint8).reshape(k // 512, 16, n))


def unpack_weight(words, scales, fmt):
    g, _, n = scales.shape
    words = np.ascontiguousarray(words).reshape(g, 128, n, -1)
    if fmt == "e4m3":
        vals = words.view(ml_dtypes.float8_e4m3fn).astype(np.float64)
    else:
        nib = np.empty((g, 128, n, 4), np.uint8)
        nib[..., 0::2] = words & 0xF
        nib[..., 1::2] = words >> 4
        vals = E2M1[nib]
    vals = vals * np.repeat(np.exp2(scales.astype(np.float64) - 127.0), 8, axis=1)[..., None]
    return vals.transpose(0, 1, 3, 2).reshape(g * 512, n)


def relu2(v):
    return np.maximum(v, 0.0) ** 2


K, T, E, C, N = 512, 640, 2, 256, 128


def by_expert(wq, xq):
    return np.concatenate([wq[e].T @ xq[:, e * C:(e + 1) * C] for e in range(E)], axis=1)


def setup_inputs():
    n = np.random.standard_normal
    s = mx_kscale(K)[:, None]
    w = [pack_weight(m, "e2m1") for m in n((E, K, N)) / np.sqrt(K) / s[None]]
    return {
        "xT": (n((K, T)) * s).astype(np.float32),
        "xr": n((N, T)).astype(np.float32),
        "w_words": np.stack([m[0] for m in w]),
        "w_scales": np.stack([m[1] for m in w]),
        "b": (0.3 * n((N, E))).astype(np.float32),
        "gate": np.tile(np.random.uniform(0.2, 1.0, E * C), (N, 1)).astype(np.float32),
        "offs": striped(np.random.permutation(T)[:E * C]),
    }


def reference(xT, xr, w_words, w_scales, b, gate, offs):
    idx = unstriped(offs)
    w = np.stack([unpack_weight(w_words[e], w_scales[e], "e2m1") for e in range(E)])
    xq = mxq(f64(xT)[:, idx], 0, "e4m3")
    y = by_expert(w, xq)
    y = relu2(y + np.repeat(f64(b), C, axis=1))
    out = f64(xr).copy()
    out[:, idx] += f64(gate) * y
    return out

@@ -1,0 +1,138 @@
+from contextlib import ExitStack
+
+import concourse.mybir as mybir
+from concourse.masks import make_identity
+
+K, T, E, C, N = 512, 640, 2, 256, 128
+FLOPS = 2 * K * N * E * C
+
+P = 128
+J = 4
+F32 = mybir.dt.float32
+BF16 = mybir.dt.bfloat16
+I32 = mybir.dt.int32
+U32 = mybir.dt.uint32
+U16 = mybir.dt.uint16
+U8 = mybir.dt.uint8
+FP8X4 = mybir.dt.float8_e4m3fn_x4
+FP4X4 = mybir.dt.float4_e2m1fn_x4
+
+ACT = mybir.ActivationFunctionType
+ALU = mybir.AluOpType
+
+CHUNKS = ((0, 256, 256), (256, 256, 160), (512, 128, 88))
+PIECES = ((0, 256), (256, 128), (384, 256))
+FLIPPED = 384
+
+
+def tile_moe_res_lin_relu2_kernel(tc, xT, xr, w_words, w_scales, b, gate, offs, out):
+    nc = tc.nc
+    with ExitStack() as ctx:
+        keep = ctx.enter_context(tc.tile_pool(name="keep", bufs=1))
+        psum = ctx.enter_context(tc.psum_pool(name="psum", bufs=1))
+
+        offsets = keep.tile([P, E * C // 16], U16, name="offsets")
+        raws = []
+        groups = []
+        for i, (t0, n, nv) in enumerate(CHUNKS):
+            raws.append(keep.tile([P, J, n], F32, name=f"raw{i}"))
+            groups.append(keep.tile([P, n, J], BF16, align_bytes=64, name=f"group{i}"))
+        codes = keep.tile([P, T], U32, align_bytes=64, name="codes")
+        scales = keep.tile([P, T], U8, align_bytes=64, name="scales")
+        ww = keep.tile([P, E, 2 * N], U8, align_bytes=64, name="ww")
+        ws = keep.tile([P, E, N], U8, align_bytes=64, name="ws")
+        bias = keep.tile([P, E], F32, name="bias")
+        gates = keep.tile([P, E * C], F32, name="gates")
+        resid = keep.tile([P, T], F32, name="resid")
+        window = keep.tile([P, T], F32, name="window")
+        relu = keep.tile([N, C], F32, name="relu")
+        identity = keep.tile([P, P], F32, name="identity")
+        flip = keep.tile([P, FLIPPED], F32, name="flip")
+        bank = psum.tile([N, E * C], F32, name="bank")
+        resid_bank = psum.tile([N, FLIPPED], F32, name="resid_bank")
+        warm = keep.tile([P, 2], F32, name="warm")
+
+        nc.vector.memset(ws[:].rearrange("p e n -> p (e n)").bitcast(I32), 0)
+        nc.vector.memset(warm[:], 0.0)
+        nc.gpsimd.memset(scales[:], 0)
+        nc.gpsimd.memset(window[:], 0.0)
+        make_identity(nc, identity[:])
+        x_rows = xT.rearrange("(p j) t -> p j t", j=J)
+        for i, (t0, n, nv) in enumerate(CHUNKS):
+            nc.sync.dma_start(out=raws[i][:], in_=x_rows[:, :, t0 : t0 + n])
+        nc.sync.dma_start(offsets[:], offs)
+        nc.sync.dma_start(out=ww[:].bitcast(I32), in_=w_words.rearrange("e a p c -> p (e a) c").bitcast(I32))
+        nc.sync.dma_start(out=gates[:], in_=gate)
+        for r in range(4):
+            nc.sync.dma_start(
+                out=ws[r:P:32, :, :].bitcast(I32),
+                in_=w_scales.rearrange("e a (q r) n -> r q (e a) n", r=4)[r].bitcast(I32),
+            )
+        nc.sync.dma_start(out=bias[:], in_=b)
+        nc.sync.dma_start(out=resid[:], in_=xr)
+        nc.scalar.activation(warm[:, 0:1], warm[:, 1:2], ACT.Relu)
+
+        for i, (t0, n, nv) in enumerate(CHUNKS):
+            nc.vector.tensor_copy(groups[i][:, 0:nv, :], raws[i][:, :, 0:nv].rearrange("p j t -> p t j"))
+            if nv < n:
+                nc.scalar.activation(groups[i][:, nv:n, :], raws[i][:, :, nv:n].rearrange("p j t -> p t j"), ACT.Copy)
+            nc.vector.quantize_mx(
+                out=codes[:, t0 : t0 + n].bitcast(FP8X4),
+                scales=scales[:, t0 : t0 + n],
+                in_=groups[i][:].rearrange("p t j -> p (t j)"),
+            )
+
+        def gather(e):
+            cols = offsets[:, e * C // 16 : (e + 1) * C // 16]
+            slot_codes = keep.tile([P, C], U32, align_bytes=64, name=f"slot_codes{e}")
+            slot_scales = keep.tile([P, C], U8, align_bytes=64, name=f"slot_scales{e}")
+            nc.vector.tensor_copy(slot_codes[:], codes[:].indirect(cols))
+            nc.vector.tensor_copy(slot_scales[:], scales[:].indirect(cols))
+            return slot_codes, slot_scales
+
+        def expert(e, slot_codes, slot_scales):
+            acc = bank[:, e * C : (e + 1) * C]
+            nc.tensor.matmul_mx(
+                out=acc,
+                lhsT=ww[:, e, :].bitcast(FP4X4),
+                lhsT_scale=ws[:, e, :],
+                rhs=slot_codes[:].bitcast(FP8X4),
+                rhs_scale=slot_scales[:],
+                start=True,
+                stop=True,
+            )
+            square = keep.tile([N, C], F32, name=f"square{e}")
+            half = C // 2 if e == 0 else C
+            for h in range(0, C, half):
+                nc.scalar.activation(relu[:, h : h + half], acc[:, h : h + half], ACT.Relu, bias=bias[:, e : e + 1])
+            for h in range(0, C, half):
+                nc.scalar.activation(square[:, h : h + half], relu[:, h : h + half], ACT.Square)
+            return square
+
+        def scatter(e, square):
+            nc.vector.tensor_tensor(
+                window[:].indirect(offsets[:, e * C // 16 : (e + 1) * C // 16]),
+                square[:],
+                gates[:, e * C : (e + 1) * C],
+                ALU.mult,
+            )
+
+        square0 = expert(0, *gather(0))
+        slots1 = gather(1)
+        scatter(0, square0)
+        scatter(1, expert(1, *slots1))
+
+        for i in range(FLIPPED // P):
+            nc.tensor.transpose(bank[:, i * P : (i + 1) * P], resid[:, i * P : (i + 1) * P], identity[:])
+        nc.scalar.copy(flip[:], bank[:, 0:FLIPPED])
+        for i in range(FLIPPED // P):
+            nc.tensor.transpose(resid_bank[:, i * P : (i + 1) * P], flip[:, i * P : (i + 1) * P], identity[:])
+
+        for i, (t0, n) in enumerate(PIECES):
+            result = keep.tile([N, n], F32, name=f"result{i}")
+            if i < 2:
+                nc.vector.tensor_tensor(result[:], resid_bank[:, t0 : t0 + n], window[:, t0 : t0 + n], ALU.add)
+            else:
+                nc.gpsimd.tensor_tensor(result[:], resid[:, t0 : t0 + n], window[:, t0 : t0 + n], ALU.add)
+            queue = nc.scalar if i == 2 else nc.sync
+            queue.dma_start(out=out[:, t0 : t0 + n], in_=result[:])

@@ -23,6 +23,7 @@ ALU = mybir.AluOpType
 CHUNKS = ((0, 256, 256), (256, 256, 160), (512, 128, 88))
 PIECES = ((0, 256), (256, 128), (384, 256))
 FLIPPED = 384
+H = C // 2
 
 
 def tile_moe_res_lin_relu2_kernel(tc, xT, xr, w_words, w_scales, b, gate, offs, out):
@@ -33,9 +34,10 @@ def tile_moe_res_lin_relu2_kernel(tc, xT, xr, w_words, w_scales, b, gate, offs, 
 
         offsets = keep.tile([P, E * C // 16], U16, name="offsets")
         raws = []
-        groups = []
         for i, (t0, n, nv) in enumerate(CHUNKS):
             raws.append(keep.tile([P, J, n], F32, name=f"raw{i}"))
+        groups = []
+        for i, (t0, n, nv) in enumerate(CHUNKS):
             groups.append(keep.tile([P, n, J], BF16, align_bytes=64, name=f"group{i}"))
         codes = keep.tile([P, T], U32, align_bytes=64, name="codes")
         scales = keep.tile([P, T], U8, align_bytes=64, name="scales")
@@ -45,15 +47,14 @@ def tile_moe_res_lin_relu2_kernel(tc, xT, xr, w_words, w_scales, b, gate, offs, 
         gates = keep.tile([P, E * C], F32, name="gates")
         resid = keep.tile([P, T], F32, name="resid")
         window = keep.tile([P, T], F32, name="window")
-        relu = keep.tile([N, C], F32, name="relu")
+        stage = keep.tile([N, FLIPPED], F32, name="stage")
         identity = keep.tile([P, P], F32, name="identity")
-        flip = keep.tile([P, FLIPPED], F32, name="flip")
-        bank = psum.tile([N, E * C], F32, name="bank")
+        bank_a = psum.tile([N, 4 * H], F32, name="bank_a")
+        bank_b = psum.tile([N, 4 * H], F32, name="bank_b")
+        bank_c = psum.tile([N, 4 * H], F32, name="bank_c")
         resid_bank = psum.tile([N, FLIPPED], F32, name="resid_bank")
-        warm = keep.tile([P, 2], F32, name="warm")
 
         nc.vector.memset(ws[:].rearrange("p e n -> p (e n)").bitcast(I32), 0)
-        nc.vector.memset(warm[:], 0.0)
         nc.gpsimd.memset(scales[:], 0)
         nc.gpsimd.memset(window[:], 0.0)
         make_identity(nc, identity[:])
@@ -70,63 +71,69 @@ def tile_moe_res_lin_relu2_kernel(tc, xT, xr, w_words, w_scales, b, gate, offs, 
             )
         nc.sync.dma_start(out=bias[:], in_=b)
         nc.sync.dma_start(out=resid[:], in_=xr)
-        nc.scalar.activation(warm[:, 0:1], warm[:, 1:2], ACT.Relu)
 
         for i, (t0, n, nv) in enumerate(CHUNKS):
-            nc.vector.tensor_copy(groups[i][:, 0:nv, :], raws[i][:, :, 0:nv].rearrange("p j t -> p t j"))
+            src = raws[i][:].rearrange("p j (c i) -> p c j i", i=4)
+            dst = groups[i][:].rearrange("p (c i) j -> p c j i", i=4)
+            nc.vector.tensor_copy(dst[:, 0 : nv // 4], src[:, 0 : nv // 4])
             if nv < n:
-                nc.scalar.activation(groups[i][:, nv:n, :], raws[i][:, :, nv:n].rearrange("p j t -> p t j"), ACT.Copy)
+                nc.scalar.activation(dst[:, nv // 4 : n // 4], src[:, nv // 4 : n // 4], ACT.Copy)
             nc.vector.quantize_mx(
                 out=codes[:, t0 : t0 + n].bitcast(FP8X4),
                 scales=scales[:, t0 : t0 + n],
                 in_=groups[i][:].rearrange("p t j -> p (t j)"),
             )
 
-        def gather(e):
-            cols = offsets[:, e * C // 16 : (e + 1) * C // 16]
-            slot_codes = keep.tile([P, C], U32, align_bytes=64, name=f"slot_codes{e}")
-            slot_scales = keep.tile([P, C], U8, align_bytes=64, name=f"slot_scales{e}")
-            nc.vector.tensor_copy(slot_codes[:], codes[:].indirect(cols))
-            nc.vector.tensor_copy(slot_scales[:], scales[:].indirect(cols))
-            return slot_codes, slot_scales
+        def entries(s0, n):
+            return offsets[:, s0 // 16 : (s0 + n) // 16]
 
-        def expert(e, slot_codes, slot_scales):
-            acc = bank[:, e * C : (e + 1) * C]
+        def gather(window_tile, dtype, s0, n, name):
+            got = keep.tile([P, n], dtype, align_bytes=64, name=name)
+            nc.vector.tensor_copy(got[:], window_tile[:].indirect(entries(s0, n)))
+            return got
+
+        def product(e, acc, slot_codes, slot_scales):
             nc.tensor.matmul_mx(
                 out=acc,
                 lhsT=ww[:, e, :].bitcast(FP4X4),
                 lhsT_scale=ws[:, e, :],
-                rhs=slot_codes[:].bitcast(FP8X4),
-                rhs_scale=slot_scales[:],
+                rhs=slot_codes.bitcast(FP8X4),
+                rhs_scale=slot_scales,
                 start=True,
                 stop=True,
             )
-            square = keep.tile([N, C], F32, name=f"square{e}")
-            half = C // 2 if e == 0 else C
-            for h in range(0, C, half):
-                nc.scalar.activation(relu[:, h : h + half], acc[:, h : h + half], ACT.Relu, bias=bias[:, e : e + 1])
-            for h in range(0, C, half):
-                nc.scalar.activation(square[:, h : h + half], relu[:, h : h + half], ACT.Square)
+
+        def relu2(e, halves, name):
+            square = keep.tile([N, len(halves) * H], F32, name=name)
+            for h, acc in enumerate(halves):
+                nc.scalar.activation(stage[:, h * H : (h + 1) * H], acc, ACT.Relu, bias=bias[:, e : e + 1])
+            for h, acc in enumerate(halves):
+                nc.scalar.activation(square[:, h * H : (h + 1) * H], stage[:, h * H : (h + 1) * H], ACT.Square)
             return square
 
-        def scatter(e, square):
-            nc.vector.tensor_tensor(
-                window[:].indirect(offsets[:, e * C // 16 : (e + 1) * C // 16]),
-                square[:],
-                gates[:, e * C : (e + 1) * C],
-                ALU.mult,
-            )
+        def scatter(s0, n, square):
+            nc.vector.tensor_tensor(window[:].indirect(entries(s0, n)), square[:], gates[:, s0 : s0 + n], ALU.mult)
 
-        square0 = expert(0, *gather(0))
-        slots1 = gather(1)
-        scatter(0, square0)
-        scatter(1, expert(1, *slots1))
+        scales_a = gather(scales, U8, 0, H, "scales_a")
+        codes_a = gather(codes, U32, 0, H, "codes_a")
+        product(0, bank_a[:, 0:H], codes_a[:], scales_a[:])
+        square_a = relu2(0, (bank_a[:, 0:H],), "square_a")
+        scales_rest = gather(scales, U8, H, H + C, "scales_rest")
+        codes_b = gather(codes, U32, H, H, "codes_b")
+        product(0, bank_b[:, 0:H], codes_b[:], scales_rest[:, 0:H])
+        square_b = relu2(0, (bank_b[:, 0:H],), "square_b")
+        codes_c = gather(codes, U32, C, C, "codes_c")
+        product(1, bank_c[:, 0:C], codes_c[:], scales_rest[:, H : H + C])
+        square_c = relu2(1, (bank_c[:, 0:H], bank_c[:, H:C]), "square_c")
+        scatter(0, H, square_a)
+        scatter(H, H, square_b)
+        scatter(C, C, square_c)
 
         for i in range(FLIPPED // P):
-            nc.tensor.transpose(bank[:, i * P : (i + 1) * P], resid[:, i * P : (i + 1) * P], identity[:])
-        nc.scalar.copy(flip[:], bank[:, 0:FLIPPED])
+            nc.tensor.transpose(bank_b[:, i * P : (i + 1) * P], resid[:, i * P : (i + 1) * P], identity[:])
+        nc.scalar.copy(stage[:], bank_b[:, 0:FLIPPED])
         for i in range(FLIPPED // P):
-            nc.tensor.transpose(resid_bank[:, i * P : (i + 1) * P], flip[:, i * P : (i + 1) * P], identity[:])
+            nc.tensor.transpose(resid_bank[:, i * P : (i + 1) * P], stage[:, i * P : (i + 1) * P], identity[:])
 
         for i, (t0, n) in enumerate(PIECES):
             result = keep.tile([N, n], F32, name=f"result{i}")

@@ -1,7 +1,6 @@
 from contextlib import ExitStack
 
 import concourse.mybir as mybir
-from concourse.masks import make_identity
 
 K, T, E, C, N = 512, 640, 2, 256, 128
 FLOPS = 2 * K * N * E * C
@@ -21,8 +20,7 @@ ACT = mybir.ActivationFunctionType
 ALU = mybir.AluOpType
 
 CHUNKS = ((0, 256, 256), (256, 256, 160), (512, 128, 88))
-PIECES = ((0, 256), (256, 128), (384, 256))
-FLIPPED = 384
+PIECES = ((0, 128), (128, 256), (384, 256))
 H = C // 2
 
 
@@ -47,29 +45,26 @@ def tile_moe_res_lin_relu2_kernel(tc, xT, xr, w_words, w_scales, b, gate, offs, 
         gates = keep.tile([P, E * C], F32, name="gates")
         resid = keep.tile([P, T], F32, name="resid")
         window = keep.tile([P, T], F32, name="window")
-        stage = keep.tile([N, FLIPPED], F32, name="stage")
-        identity = keep.tile([P, P], F32, name="identity")
+        stage = keep.tile([N, C], F32, name="stage")
         bank_a = psum.tile([N, 4 * H], F32, name="bank_a")
         bank_b = psum.tile([N, 4 * H], F32, name="bank_b")
         bank_c = psum.tile([N, 4 * H], F32, name="bank_c")
-        resid_bank = psum.tile([N, FLIPPED], F32, name="resid_bank")
 
-        nc.vector.memset(ws[:].rearrange("p e n -> p (e n)").bitcast(I32), 0)
+        nc.gpsimd.memset(ws[:].rearrange("p e n -> p (e n)").bitcast(I32), 0)
         nc.gpsimd.memset(scales[:], 0)
         nc.gpsimd.memset(window[:], 0.0)
-        make_identity(nc, identity[:])
         x_rows = xT.rearrange("(p j) t -> p j t", j=J)
         for i, (t0, n, nv) in enumerate(CHUNKS):
             nc.sync.dma_start(out=raws[i][:], in_=x_rows[:, :, t0 : t0 + n])
         nc.sync.dma_start(offsets[:], offs)
         nc.sync.dma_start(out=ww[:].bitcast(I32), in_=w_words.rearrange("e a p c -> p (e a) c").bitcast(I32))
-        nc.sync.dma_start(out=gates[:], in_=gate)
         for r in range(4):
             nc.sync.dma_start(
                 out=ws[r:P:32, :, :].bitcast(I32),
                 in_=w_scales.rearrange("e a (q r) n -> r q (e a) n", r=4)[r].bitcast(I32),
             )
         nc.sync.dma_start(out=bias[:], in_=b)
+        nc.sync.dma_start(out=gates[:], in_=gate)
         nc.sync.dma_start(out=resid[:], in_=xr)
 
         for i, (t0, n, nv) in enumerate(CHUNKS):
@@ -129,17 +124,8 @@ def tile_moe_res_lin_relu2_kernel(tc, xT, xr, w_words, w_scales, b, gate, offs, 
         scatter(H, H, square_b)
         scatter(C, C, square_c)
 
-        for i in range(FLIPPED // P):
-            nc.tensor.transpose(bank_b[:, i * P : (i + 1) * P], resid[:, i * P : (i + 1) * P], identity[:])
-        nc.scalar.copy(stage[:], bank_b[:, 0:FLIPPED])
-        for i in range(FLIPPED // P):
-            nc.tensor.transpose(resid_bank[:, i * P : (i + 1) * P], stage[:, i * P : (i + 1) * P], identity[:])
-
         for i, (t0, n) in enumerate(PIECES):
             result = keep.tile([N, n], F32, name=f"result{i}")
-            if i < 2:
-                nc.vector.tensor_tensor(result[:], resid_bank[:, t0 : t0 + n], window[:, t0 : t0 + n], ALU.add)
-            else:
-                nc.gpsimd.tensor_tensor(result[:], resid[:, t0 : t0 + n], window[:, t0 : t0 + n], ALU.add)
-            queue = nc.scalar if i == 2 else nc.sync
+            nc.vector.tensor_tensor(result[:], resid[:, t0 : t0 + n], window[:, t0 : t0 + n], ALU.add)
+            queue = nc.scalar if i == 1 else nc.sync
             queue.dma_start(out=out[:, t0 : t0 + n], in_=result[:])

@@ -1,6 +1,7 @@
 from contextlib import ExitStack
 
 import concourse.mybir as mybir
+from concourse.masks import make_identity
 
 K, T, E, C, N = 512, 640, 2, 256, 128
 FLOPS = 2 * K * N * E * C
@@ -20,7 +21,8 @@ ACT = mybir.ActivationFunctionType
 ALU = mybir.AluOpType
 
 CHUNKS = ((0, 256, 256), (256, 256, 160), (512, 128, 88))
-PIECES = ((0, 128), (128, 256), (384, 256))
+PIECES = ((0, 256), (256, 128), (384, 256))
+FLIPPED = 384
 H = C // 2
 
 
@@ -28,6 +30,7 @@ def tile_moe_res_lin_relu2_kernel(tc, xT, xr, w_words, w_scales, b, gate, offs, 
     nc = tc.nc
     with ExitStack() as ctx:
         keep = ctx.enter_context(tc.tile_pool(name="keep", bufs=1))
+        turns = ctx.enter_context(tc.tile_pool(name="turns", bufs=1))
         psum = ctx.enter_context(tc.psum_pool(name="psum", bufs=1))
 
         offsets = keep.tile([P, E * C // 16], U16, name="offsets")
@@ -45,26 +48,29 @@ def tile_moe_res_lin_relu2_kernel(tc, xT, xr, w_words, w_scales, b, gate, offs, 
         gates = keep.tile([P, E * C], F32, name="gates")
         resid = keep.tile([P, T], F32, name="resid")
         window = keep.tile([P, T], F32, name="window")
-        stage = keep.tile([N, C], F32, name="stage")
+        identity = keep.tile([P, P], F32, name="identity")
         bank_a = psum.tile([N, 4 * H], F32, name="bank_a")
         bank_b = psum.tile([N, 4 * H], F32, name="bank_b")
         bank_c = psum.tile([N, 4 * H], F32, name="bank_c")
+        bank_d = psum.tile([N, 4 * H], F32, name="bank_d")
+        resid_bank = psum.tile([N, FLIPPED], F32, name="resid_bank")
 
-        nc.gpsimd.memset(ws[:].rearrange("p e n -> p (e n)").bitcast(I32), 0)
+        nc.vector.memset(ws[:].rearrange("p e n -> p (e n)").bitcast(I32), 0)
         nc.gpsimd.memset(scales[:], 0)
         nc.gpsimd.memset(window[:], 0.0)
+        make_identity(nc, identity[:])
         x_rows = xT.rearrange("(p j) t -> p j t", j=J)
         for i, (t0, n, nv) in enumerate(CHUNKS):
             nc.sync.dma_start(out=raws[i][:], in_=x_rows[:, :, t0 : t0 + n])
         nc.sync.dma_start(offsets[:], offs)
         nc.sync.dma_start(out=ww[:].bitcast(I32), in_=w_words.rearrange("e a p c -> p (e a) c").bitcast(I32))
+        nc.sync.dma_start(out=gates[:], in_=gate)
         for r in range(4):
             nc.sync.dma_start(
                 out=ws[r:P:32, :, :].bitcast(I32),
                 in_=w_scales.rearrange("e a (q r) n -> r q (e a) n", r=4)[r].bitcast(I32),
             )
         nc.sync.dma_start(out=bias[:], in_=b)
-        nc.sync.dma_start(out=gates[:], in_=gate)
         nc.sync.dma_start(out=resid[:], in_=xr)
 
         for i, (t0, n, nv) in enumerate(CHUNKS):
@@ -98,13 +104,8 @@ def tile_moe_res_lin_relu2_kernel(tc, xT, xr, w_words, w_scales, b, gate, offs, 
                 stop=True,
             )
 
-        def relu2(e, halves, name):
-            square = keep.tile([N, len(halves) * H], F32, name=name)
-            for h, acc in enumerate(halves):
-                nc.scalar.activation(stage[:, h * H : (h + 1) * H], acc, ACT.Relu, bias=bias[:, e : e + 1])
-            for h, acc in enumerate(halves):
-                nc.scalar.activation(square[:, h * H : (h + 1) * H], stage[:, h * H : (h + 1) * H], ACT.Square)
-            return square
+        def relu(e, dst, acc):
+            nc.scalar.activation(dst, acc, ACT.Relu, bias=bias[:, e : e + 1])
 
         def scatter(s0, n, square):
             nc.vector.tensor_tensor(window[:].indirect(entries(s0, n)), square[:], gates[:, s0 : s0 + n], ALU.mult)
@@ -112,20 +113,48 @@ def tile_moe_res_lin_relu2_kernel(tc, xT, xr, w_words, w_scales, b, gate, offs, 
         scales_a = gather(scales, U8, 0, H, "scales_a")
         codes_a = gather(codes, U32, 0, H, "codes_a")
         product(0, bank_a[:, 0:H], codes_a[:], scales_a[:])
-        square_a = relu2(0, (bank_a[:, 0:H],), "square_a")
-        scales_rest = gather(scales, U8, H, H + C, "scales_rest")
+        relu_a = turns.tile([N, H], F32, align_bytes=64, offset=1792, name="relu_a")
+        for h in (0, H // 2):
+            relu(0, relu_a[:, h : h + H // 2], bank_a[:, h : h + H // 2])
+        square_a = keep.tile([N, H], F32, name="square_a")
+        for h in (0, H // 2):
+            nc.scalar.activation(square_a[:, h : h + H // 2], relu_a[:, h : h + H // 2], ACT.Square)
+
+        scales_bc = gather(scales, U8, H, C, "scales_bc")
         codes_b = gather(codes, U32, H, H, "codes_b")
-        product(0, bank_b[:, 0:H], codes_b[:], scales_rest[:, 0:H])
-        square_b = relu2(0, (bank_b[:, 0:H],), "square_b")
-        codes_c = gather(codes, U32, C, C, "codes_c")
-        product(1, bank_c[:, 0:C], codes_c[:], scales_rest[:, H : H + C])
-        square_c = relu2(1, (bank_c[:, 0:H], bank_c[:, H:C]), "square_c")
+        product(0, bank_b[:, 0:H], codes_b[:], scales_bc[:, 0:H])
+        codes_c = gather(codes, U32, 2 * H, H, "codes_c")
+        product(1, bank_c[:, 0:H], codes_c[:], scales_bc[:, H:C])
+        stage = turns.tile([N, C], F32, align_bytes=64, offset=1024, name="stage")
+        square_bc = keep.tile([N, C], F32, name="square_bc")
+        relu(0, stage[:, 0:H], bank_b[:, 0:H])
+        relu(1, stage[:, H:C], bank_c[:, 0:H])
+        nc.scalar.activation(square_bc[:, 0:H], stage[:, 0:H], ACT.Square)
+        nc.scalar.activation(square_bc[:, H:C], stage[:, H:C], ACT.Square)
+
+        scales_d = gather(scales, U8, 3 * H, H, "scales_d")
         scatter(0, H, square_a)
-        scatter(H, H, square_b)
-        scatter(C, C, square_c)
+        codes_d = turns.tile([P, H], U32, align_bytes=64, offset=2048, name="codes_d")
+        nc.vector.tensor_copy(codes_d[:], codes[:].indirect(entries(3 * H, H)))
+        for i in range(FLIPPED // P):
+            nc.tensor.transpose(bank_a[:, i * P : (i + 1) * P], resid[:, i * P : (i + 1) * P], identity[:])
+        flip = turns.tile([P, FLIPPED], F32, align_bytes=64, offset=0, name="flip")
+        nc.scalar.copy(flip[:], bank_a[:, 0:FLIPPED])
+        product(1, bank_d[:, 0:H], codes_d[:], scales_d[:])
+        for i in range(FLIPPED // P):
+            nc.tensor.transpose(resid_bank[:, i * P : (i + 1) * P], flip[:, i * P : (i + 1) * P], identity[:])
+        relu_d = turns.tile([N, H], F32, align_bytes=64, offset=1536, name="relu_d")
+        relu(1, relu_d[:], bank_d[:, 0:H])
+        square_d = keep.tile([N, H], F32, name="square_d")
+        nc.scalar.activation(square_d[:], relu_d[:], ACT.Square)
+        scatter(H, C, square_bc)
+        scatter(3 * H, H, square_d)
 
         for i, (t0, n) in enumerate(PIECES):
             result = keep.tile([N, n], F32, name=f"result{i}")
-            nc.vector.tensor_tensor(result[:], resid[:, t0 : t0 + n], window[:, t0 : t0 + n], ALU.add)
-            queue = nc.scalar if i == 1 else nc.sync
+            if i < 2:
+                nc.vector.tensor_tensor(result[:], resid_bank[:, t0 : t0 + n], window[:, t0 : t0 + n], ALU.add)
+            else:
+                nc.gpsimd.tensor_tensor(result[:], resid[:, t0 : t0 + n], window[:, t0 : t0 + n], ALU.add)
+            queue = nc.scalar if i == 2 else nc.sync
             queue.dma_start(out=out[:, t0 : t0 + n], in_=result[:])

@@ -21,7 +21,7 @@ ACT = mybir.ActivationFunctionType
 ALU = mybir.AluOpType
 
 CHUNKS = ((0, 256, 256), (256, 256, 160), (512, 128, 88))
-PIECES = ((0, 256), (256, 128), (384, 256))
+PIECES = ((0, 128), (128, 256), (384, 128), (512, 128))
 FLIPPED = 384
 H = C // 2
 
@@ -55,7 +55,7 @@ def tile_moe_res_lin_relu2_kernel(tc, xT, xr, w_words, w_scales, b, gate, offs, 
         bank_d = psum.tile([N, 4 * H], F32, name="bank_d")
         resid_bank = psum.tile([N, FLIPPED], F32, name="resid_bank")
 
-        nc.vector.memset(ws[:].rearrange("p e n -> p (e n)").bitcast(I32), 0)
+        nc.gpsimd.memset(ws[:].rearrange("p e n -> p (e n)").bitcast(I32), 0)
         nc.gpsimd.memset(scales[:], 0)
         nc.gpsimd.memset(window[:], 0.0)
         make_identity(nc, identity[:])
@@ -64,12 +64,12 @@ def tile_moe_res_lin_relu2_kernel(tc, xT, xr, w_words, w_scales, b, gate, offs, 
             nc.sync.dma_start(out=raws[i][:], in_=x_rows[:, :, t0 : t0 + n])
         nc.sync.dma_start(offsets[:], offs)
         nc.sync.dma_start(out=ww[:].bitcast(I32), in_=w_words.rearrange("e a p c -> p (e a) c").bitcast(I32))
-        nc.sync.dma_start(out=gates[:], in_=gate)
         for r in range(4):
             nc.sync.dma_start(
                 out=ws[r:P:32, :, :].bitcast(I32),
                 in_=w_scales.rearrange("e a (q r) n -> r q (e a) n", r=4)[r].bitcast(I32),
             )
+        nc.sync.dma_start(out=gates[:], in_=gate)
         nc.sync.dma_start(out=bias[:], in_=b)
         nc.sync.dma_start(out=resid[:], in_=xr)
 
@@ -156,5 +156,5 @@ def tile_moe_res_lin_relu2_kernel(tc, xT, xr, w_words, w_scales, b, gate, offs, 
                 nc.vector.tensor_tensor(result[:], resid_bank[:, t0 : t0 + n], window[:, t0 : t0 + n], ALU.add)
             else:
                 nc.gpsimd.tensor_tensor(result[:], resid[:, t0 : t0 + n], window[:, t0 : t0 + n], ALU.add)
-            queue = nc.scalar if i == 2 else nc.sync
+            queue = nc.scalar if i >= 2 else nc.sync
             queue.dma_start(out=out[:, t0 : t0 + n], in_=result[:])

@@ -8,6 +8,10 @@ FLOPS = 2 * K * N * E * C
 
 P = 128
 J = 4
+Q = C // 2
+BANK = 512
+LIST = 16
+LINE = 4
 F32 = mybir.dt.float32
 BF16 = mybir.dt.bfloat16
 I32 = mybir.dt.int32
@@ -21,140 +25,133 @@ ACT = mybir.ActivationFunctionType
 ALU = mybir.AluOpType
 
 CHUNKS = ((0, 256, 256), (256, 256, 160), (512, 128, 88))
-PIECES = ((0, 128), (128, 256), (384, 128), (512, 128))
-FLIPPED = 384
-H = C // 2
+TURNED = 512
+PIECES = ((0, 128), (512, 128), (128, 128), (256, 256))
 
 
 def tile_moe_res_lin_relu2_kernel(tc, xT, xr, w_words, w_scales, b, gate, offs, out):
     nc = tc.nc
     with ExitStack() as ctx:
         keep = ctx.enter_context(tc.tile_pool(name="keep", bufs=1))
-        turns = ctx.enter_context(tc.tile_pool(name="turns", bufs=1))
+        scratch = ctx.enter_context(tc.tile_pool(name="scratch", bufs=1))
         psum = ctx.enter_context(tc.psum_pool(name="psum", bufs=1))
 
-        offsets = keep.tile([P, E * C // 16], U16, name="offsets")
-        raws = []
-        for i, (t0, n, nv) in enumerate(CHUNKS):
-            raws.append(keep.tile([P, J, n], F32, name=f"raw{i}"))
-        groups = []
-        for i, (t0, n, nv) in enumerate(CHUNKS):
-            groups.append(keep.tile([P, n, J], BF16, align_bytes=64, name=f"group{i}"))
+        offsets = keep.tile([P, E * C // LIST], U16, name="offsets")
+        raws = [keep.tile([P, J, n], F32, name=f"raw{t0}") for t0, n, on_vector in CHUNKS]
+        rounded = [keep.tile([P, n, J], BF16, align_bytes=64, name=f"rounded{t0}") for t0, n, on_vector in CHUNKS]
         codes = keep.tile([P, T], U32, align_bytes=64, name="codes")
         scales = keep.tile([P, T], U8, align_bytes=64, name="scales")
-        ww = keep.tile([P, E, 2 * N], U8, align_bytes=64, name="ww")
-        ws = keep.tile([P, E, N], U8, align_bytes=64, name="ws")
+        w_codes = keep.tile([P, E, 2 * N], U8, align_bytes=64, name="w_codes")
+        w_scale = keep.tile([P, E, N], U8, align_bytes=64, name="w_scale")
         bias = keep.tile([P, E], F32, name="bias")
         gates = keep.tile([P, E * C], F32, name="gates")
         resid = keep.tile([P, T], F32, name="resid")
-        window = keep.tile([P, T], F32, name="window")
+        main = keep.tile([P, T], F32, name="main")
+        side = keep.tile([P, T], F32, name="side")
         identity = keep.tile([P, P], F32, name="identity")
-        bank_a = psum.tile([N, 4 * H], F32, name="bank_a")
-        bank_b = psum.tile([N, 4 * H], F32, name="bank_b")
-        bank_c = psum.tile([N, 4 * H], F32, name="bank_c")
-        bank_d = psum.tile([N, 4 * H], F32, name="bank_d")
-        resid_bank = psum.tile([N, FLIPPED], F32, name="resid_bank")
+        banks = [psum.tile([N, BANK], F32, name=f"bank{i}") for i in range(E * C // Q)]
 
-        nc.gpsimd.memset(ws[:].rearrange("p e n -> p (e n)").bitcast(I32), 0)
+        nc.gpsimd.memset(w_scale[:].rearrange("p e n -> p (e n)").bitcast(I32), 0)
         nc.gpsimd.memset(scales[:], 0)
-        nc.gpsimd.memset(window[:], 0.0)
+        nc.gpsimd.memset(main[:], 0.0)
+        nc.vector.memset(side[:], 0.0)
         make_identity(nc, identity[:])
+
         x_rows = xT.rearrange("(p j) t -> p j t", j=J)
-        for i, (t0, n, nv) in enumerate(CHUNKS):
-            nc.sync.dma_start(out=raws[i][:], in_=x_rows[:, :, t0 : t0 + n])
+        for raw, (t0, n, on_vector) in zip(raws, CHUNKS):
+            nc.sync.dma_start(out=raw[:], in_=x_rows[:, :, t0 : t0 + n])
         nc.sync.dma_start(offsets[:], offs)
-        nc.sync.dma_start(out=ww[:].bitcast(I32), in_=w_words.rearrange("e a p c -> p (e a) c").bitcast(I32))
+        nc.sync.dma_start(out=w_codes[:].bitcast(I32), in_=w_words.rearrange("e a p c -> p (e a) c").bitcast(I32))
         for r in range(4):
             nc.sync.dma_start(
-                out=ws[r:P:32, :, :].bitcast(I32),
-                in_=w_scales.rearrange("e a (q r) n -> r q (e a) n", r=4)[r].bitcast(I32),
+                out=w_scale[r:P:32, :, :].bitcast(I32),
+                in_=w_scales.rearrange("e a (g r) n -> r g (e a) n", r=4)[r].bitcast(I32),
             )
         nc.sync.dma_start(out=gates[:], in_=gate)
         nc.sync.dma_start(out=bias[:], in_=b)
         nc.sync.dma_start(out=resid[:], in_=xr)
 
-        for i, (t0, n, nv) in enumerate(CHUNKS):
-            src = raws[i][:].rearrange("p j (c i) -> p c j i", i=4)
-            dst = groups[i][:].rearrange("p (c i) j -> p c j i", i=4)
-            nc.vector.tensor_copy(dst[:, 0 : nv // 4], src[:, 0 : nv // 4])
-            if nv < n:
-                nc.scalar.activation(dst[:, nv // 4 : n // 4], src[:, nv // 4 : n // 4], ACT.Copy)
+        for raw, tokens, (t0, n, on_vector) in zip(raws, rounded, CHUNKS):
+            src = raw[:].rearrange("p j (c i) -> p c j i", i=LINE)
+            dst = tokens[:].rearrange("p (c i) j -> p c j i", i=LINE)
+            cut = on_vector // LINE
+            nc.vector.tensor_copy(dst[:, 0:cut], src[:, 0:cut])
+            if on_vector < n:
+                nc.scalar.activation(dst[:, cut : n // LINE], src[:, cut : n // LINE], ACT.Copy)
             nc.vector.quantize_mx(
                 out=codes[:, t0 : t0 + n].bitcast(FP8X4),
                 scales=scales[:, t0 : t0 + n],
-                in_=groups[i][:].rearrange("p t j -> p (t j)"),
+                in_=tokens[:].rearrange("p t j -> p (t j)"),
             )
 
         def entries(s0, n):
-            return offsets[:, s0 // 16 : (s0 + n) // 16]
+            return offsets[:, s0 // LIST : (s0 + n) // LIST]
 
-        def gather(window_tile, dtype, s0, n, name):
+        def gather(table, dtype, s0, n, name):
             got = keep.tile([P, n], dtype, align_bytes=64, name=name)
-            nc.vector.tensor_copy(got[:], window_tile[:].indirect(entries(s0, n)))
+            nc.vector.tensor_copy(got[:], table[:].indirect(entries(s0, n)))
             return got
 
-        def product(e, acc, slot_codes, slot_scales):
+        def product(quarter, slot_scales):
+            e = quarter * Q // C
+            slot_codes = gather(codes, U32, quarter * Q, Q, f"slot_codes{quarter}")
             nc.tensor.matmul_mx(
-                out=acc,
-                lhsT=ww[:, e, :].bitcast(FP4X4),
-                lhsT_scale=ws[:, e, :],
-                rhs=slot_codes.bitcast(FP8X4),
+                out=banks[quarter][:, 0:Q],
+                lhsT=w_codes[:, e, :].bitcast(FP4X4),
+                lhsT_scale=w_scale[:, e, :],
+                rhs=slot_codes[:].bitcast(FP8X4),
                 rhs_scale=slot_scales,
                 start=True,
                 stop=True,
             )
 
-        def relu(e, dst, acc):
-            nc.scalar.activation(dst, acc, ACT.Relu, bias=bias[:, e : e + 1])
+        def relu2(e, sums, name):
+            width = sums[0].shape[1]
+            relu = scratch.tile([N, len(sums) * width], F32, name=f"relu_{name}", tag="scratch")
+            square = keep.tile([N, len(sums) * width], F32, name=f"square_{name}")
+            for i, acc in enumerate(sums):
+                nc.scalar.activation(relu[:, i * width : (i + 1) * width], acc, ACT.Relu, bias=bias[:, e : e + 1])
+            for i in range(len(sums)):
+                nc.scalar.activation(square[:, i * width : (i + 1) * width], relu[:, i * width : (i + 1) * width], ACT.Square)
+            return square
 
-        def scatter(s0, n, square):
+        def scatter(window, s0, n, square):
             nc.vector.tensor_tensor(window[:].indirect(entries(s0, n)), square[:], gates[:, s0 : s0 + n], ALU.mult)
 
-        scales_a = gather(scales, U8, 0, H, "scales_a")
-        codes_a = gather(codes, U32, 0, H, "codes_a")
-        product(0, bank_a[:, 0:H], codes_a[:], scales_a[:])
-        relu_a = turns.tile([N, H], F32, align_bytes=64, offset=1792, name="relu_a")
-        for h in (0, H // 2):
-            relu(0, relu_a[:, h : h + H // 2], bank_a[:, h : h + H // 2])
-        square_a = keep.tile([N, H], F32, name="square_a")
-        for h in (0, H // 2):
-            nc.scalar.activation(square_a[:, h : h + H // 2], relu_a[:, h : h + H // 2], ACT.Square)
+        def turn(dst, src, start, stop):
+            nc.tensor.matmul(dst, src, identity[:], start=start, stop=stop, is_transpose=True)
 
-        scales_bc = gather(scales, U8, H, C, "scales_bc")
-        codes_b = gather(codes, U32, H, H, "codes_b")
-        product(0, bank_b[:, 0:H], codes_b[:], scales_bc[:, 0:H])
-        codes_c = gather(codes, U32, 2 * H, H, "codes_c")
-        product(1, bank_c[:, 0:H], codes_c[:], scales_bc[:, H:C])
-        stage = turns.tile([N, C], F32, align_bytes=64, offset=1024, name="stage")
-        square_bc = keep.tile([N, C], F32, name="square_bc")
-        relu(0, stage[:, 0:H], bank_b[:, 0:H])
-        relu(1, stage[:, H:C], bank_c[:, 0:H])
-        nc.scalar.activation(square_bc[:, 0:H], stage[:, 0:H], ACT.Square)
-        nc.scalar.activation(square_bc[:, H:C], stage[:, H:C], ACT.Square)
+        product(0, gather(scales, U8, 0, Q, "slot_scales0")[:])
+        first = relu2(0, (banks[0][:, 0 : Q // 2], banks[0][:, Q // 2 : Q]), "first")
+        product(1, gather(scales, U8, Q, Q, "slot_scales1")[:])
+        second = relu2(0, (banks[1][:, 0:Q],), "second")
+        last_scales = gather(scales, U8, C, C, "slot_scales23")
+        product(2, last_scales[:, 0:Q])
+        product(3, last_scales[:, Q:C])
+        last = relu2(1, (banks[2][:, 0:Q], banks[3][:, 0:Q]), "last")
 
-        scales_d = gather(scales, U8, 3 * H, H, "scales_d")
-        scatter(0, H, square_a)
-        codes_d = turns.tile([P, H], U32, align_bytes=64, offset=2048, name="codes_d")
-        nc.vector.tensor_copy(codes_d[:], codes[:].indirect(entries(3 * H, H)))
-        for i in range(FLIPPED // P):
-            nc.tensor.transpose(bank_a[:, i * P : (i + 1) * P], resid[:, i * P : (i + 1) * P], identity[:])
-        flip = turns.tile([P, FLIPPED], F32, align_bytes=64, offset=0, name="flip")
-        nc.scalar.copy(flip[:], bank_a[:, 0:FLIPPED])
-        product(1, bank_d[:, 0:H], codes_d[:], scales_d[:])
-        for i in range(FLIPPED // P):
-            nc.tensor.transpose(resid_bank[:, i * P : (i + 1) * P], flip[:, i * P : (i + 1) * P], identity[:])
-        relu_d = turns.tile([N, H], F32, align_bytes=64, offset=1536, name="relu_d")
-        relu(1, relu_d[:], bank_d[:, 0:H])
-        square_d = keep.tile([N, H], F32, name="square_d")
-        nc.scalar.activation(square_d[:], relu_d[:], ACT.Square)
-        scatter(H, C, square_bc)
-        scatter(3 * H, H, square_d)
+        for i, bank in enumerate(banks):
+            turn(bank[:, 0:P], resid[:, i * P : (i + 1) * P], True, False)
+        scatter(main, 0, Q, first)
+        scatter(side, Q, Q, second)
+        scatter(main, C, C, last)
+        flipped = scratch.tile([P, TURNED], F32, name="flipped", tag="scratch")
+        for i, bank in enumerate(banks):
+            turn(bank[:, 0:P], side[:, i * P : (i + 1) * P], False, True)
+            nc.scalar.copy(flipped[:, i * P : (i + 1) * P], bank[:, 0:P])
+        partial = {}
+        for t0, n in PIECES:
+            if t0 < TURNED:
+                partial[t0] = psum.tile([N, BANK], F32, name=f"partial{t0}")
+                for col in range(0, n, P):
+                    turn(partial[t0][:, col : col + P], flipped[:, t0 + col : t0 + col + P], True, True)
+
+        partial[TURNED] = keep.tile([N, T - TURNED], F32, name="partial_sbuf")
+        nc.vector.tensor_tensor(partial[TURNED][:], resid[:, TURNED:T], side[:, TURNED:T], ALU.add)
 
         for i, (t0, n) in enumerate(PIECES):
-            result = keep.tile([N, n], F32, name=f"result{i}")
-            if i < 2:
-                nc.vector.tensor_tensor(result[:], resid_bank[:, t0 : t0 + n], window[:, t0 : t0 + n], ALU.add)
-            else:
-                nc.gpsimd.tensor_tensor(result[:], resid[:, t0 : t0 + n], window[:, t0 : t0 + n], ALU.add)
-            queue = nc.scalar if i >= 2 else nc.sync
+            result = keep.tile([N, n], F32, name=f"result{t0}")
+            engine = nc.vector if t0 < TURNED else nc.gpsimd
+            engine.tensor_tensor(result[:], partial[t0][:, 0:n], main[:, t0 : t0 + n], ALU.add)
+            queue = nc.scalar if i % 2 else nc.sync
             queue.dma_start(out=out[:, t0 : t0 + n], in_=result[:])

@@ -12,6 +12,8 @@ Q = C // 2
 BANK = 512
 LIST = 16
 LINE = 4
+QUADRANT = 32
+ROWS = 4
 F32 = mybir.dt.float32
 BF16 = mybir.dt.bfloat16
 I32 = mybir.dt.int32
@@ -62,10 +64,10 @@ def tile_moe_res_lin_relu2_kernel(tc, xT, xr, w_words, w_scales, b, gate, offs, 
             nc.sync.dma_start(out=raw[:], in_=x_rows[:, :, t0 : t0 + n])
         nc.sync.dma_start(offsets[:], offs)
         nc.sync.dma_start(out=w_codes[:].bitcast(I32), in_=w_words.rearrange("e a p c -> p (e a) c").bitcast(I32))
-        for r in range(4):
+        for r in range(ROWS):
             nc.sync.dma_start(
-                out=w_scale[r:P:32, :, :].bitcast(I32),
-                in_=w_scales.rearrange("e a (g r) n -> r g (e a) n", r=4)[r].bitcast(I32),
+                out=w_scale[r:P:QUADRANT, :, :].bitcast(I32),
+                in_=w_scales.rearrange("e a (g r) n -> r g (e a) n", r=ROWS)[r].bitcast(I32),
             )
         nc.sync.dma_start(out=gates[:], in_=gate)
         nc.sync.dma_start(out=bias[:], in_=b)
@@ -92,14 +94,12 @@ def tile_moe_res_lin_relu2_kernel(tc, xT, xr, w_words, w_scales, b, gate, offs, 
             nc.vector.tensor_copy(got[:], table[:].indirect(entries(s0, n)))
             return got
 
-        def product(quarter, slot_scales):
-            e = quarter * Q // C
-            slot_codes = gather(codes, U32, quarter * Q, Q, f"slot_codes{quarter}")
+        def product(e, acc, slot_codes, slot_scales):
             nc.tensor.matmul_mx(
-                out=banks[quarter][:, 0:Q],
+                out=acc,
                 lhsT=w_codes[:, e, :].bitcast(FP4X4),
                 lhsT_scale=w_scale[:, e, :],
-                rhs=slot_codes[:].bitcast(FP8X4),
+                rhs=slot_codes.bitcast(FP8X4),
                 rhs_scale=slot_scales,
                 start=True,
                 stop=True,
@@ -107,12 +107,12 @@ def tile_moe_res_lin_relu2_kernel(tc, xT, xr, w_words, w_scales, b, gate, offs, 
 
         def relu2(e, sums, name):
             width = sums[0].shape[1]
-            relu = scratch.tile([N, len(sums) * width], F32, name=f"relu_{name}", tag="scratch")
-            square = keep.tile([N, len(sums) * width], F32, name=f"square_{name}")
-            for i, acc in enumerate(sums):
-                nc.scalar.activation(relu[:, i * width : (i + 1) * width], acc, ACT.Relu, bias=bias[:, e : e + 1])
-            for i in range(len(sums)):
-                nc.scalar.activation(square[:, i * width : (i + 1) * width], relu[:, i * width : (i + 1) * width], ACT.Square)
+            relus = [scratch.tile([N, width], F32, name=f"relu_{name}{i}", tag=f"scratch{i}") for i in range(2)]
+            square = keep.tile([N, 2 * width], F32, name=f"square_{name}")
+            for relu, acc in zip(relus, sums):
+                nc.scalar.activation(relu[:], acc, ACT.Relu, bias=bias[:, e : e + 1])
+            for i, relu in enumerate(relus):
+                nc.scalar.activation(square[:, i * width : (i + 1) * width], relu[:], ACT.Square)
             return square
 
         def scatter(window, s0, n, square):
@@ -121,13 +121,16 @@ def tile_moe_res_lin_relu2_kernel(tc, xT, xr, w_words, w_scales, b, gate, offs, 
         def turn(dst, src, start, stop):
             nc.tensor.matmul(dst, src, identity[:], start=start, stop=stop, is_transpose=True)
 
-        product(0, gather(scales, U8, 0, Q, "slot_scales0")[:])
+        first_scales = gather(scales, U8, 0, Q, "first_scales")
+        product(0, banks[0][:, 0:Q], gather(codes, U32, 0, Q, "first_codes")[:], first_scales[:])
         first = relu2(0, (banks[0][:, 0 : Q // 2], banks[0][:, Q // 2 : Q]), "first")
-        product(1, gather(scales, U8, Q, Q, "slot_scales1")[:])
-        second = relu2(0, (banks[1][:, 0:Q],), "second")
+        second_scales = gather(scales, U8, Q, Q, "second_scales")
+        product(0, banks[1][:, 0:Q], gather(codes, U32, Q, Q, "second_codes")[:], second_scales[:])
+        second = relu2(0, (banks[1][:, 0 : Q // 2], banks[1][:, Q // 2 : Q]), "second")
         last_scales = gather(scales, U8, C, C, "slot_scales23")
-        product(2, last_scales[:, 0:Q])
-        product(3, last_scales[:, Q:C])
+        last_codes = gather(codes, U32, C, C, "last_codes")
+        product(1, banks[2][:, 0:Q], last_codes[:, 0:Q], last_scales[:, 0:Q])
+        product(1, banks[3][:, 0:Q], last_codes[:, Q:C], last_scales[:, Q:C])
         last = relu2(1, (banks[2][:, 0:Q], banks[3][:, 0:Q]), "last")
 
         for i, bank in enumerate(banks):
@@ -135,7 +138,7 @@ def tile_moe_res_lin_relu2_kernel(tc, xT, xr, w_words, w_scales, b, gate, offs, 
         scatter(main, 0, Q, first)
         scatter(side, Q, Q, second)
         scatter(main, C, C, last)
-        flipped = scratch.tile([P, TURNED], F32, name="flipped", tag="scratch")
+        flipped = scratch.tile([P, TURNED], F32, name="flipped", tag="scratch1")
         for i, bank in enumerate(banks):
             turn(bank[:, 0:P], side[:, i * P : (i + 1) * P], False, True)
             nc.scalar.copy(flipped[:, i * P : (i + 1) * P], bank[:, 0:P])

@@ -53,9 +53,8 @@ def tile_moe_res_lin_relu2_kernel(tc, xT, xr, w_words, w_scales, b, gate, offs, 
         identity = keep.tile([P, P], F32, name="identity")
         banks = [psum.tile([N, BANK], F32, name=f"bank{i}") for i in range(E * C // Q)]
 
-        nc.gpsimd.memset(w_scale[:].rearrange("p e n -> p (e n)").bitcast(I32), 0)
-        nc.gpsimd.memset(scales[:], 0)
-        nc.gpsimd.memset(main[:], 0.0)
+        nc.vector.memset(scales[:].bitcast(I32), 0)
+        nc.vector.memset(main[:], 0.0)
         nc.vector.memset(side[:], 0.0)
         make_identity(nc, identity[:])
 

@@ -151,9 +151,9 @@ def tile_moe_res_lin_relu2_kernel(tc, xT, xr, w_words, w_scales, b, gate, offs, 
         partial[TURNED] = keep.tile([N, T - TURNED], F32, name="partial_sbuf")
         nc.vector.tensor_tensor(partial[TURNED][:], resid[:, TURNED:T], side[:, TURNED:T], ALU.add)
 
-        for i, (t0, n) in enumerate(PIECES):
+        for t0, n in PIECES:
             result = keep.tile([N, n], F32, name=f"result{t0}")
             engine = nc.vector if t0 < TURNED else nc.gpsimd
             engine.tensor_tensor(result[:], partial[t0][:, 0:n], main[:, t0 : t0 + n], ALU.add)
-            queue = nc.scalar if i % 2 else nc.sync
+            queue = nc.sync if t0 < TURNED else nc.scalar
             queue.dma_start(out=out[:, t0 : t0 + n], in_=result[:])

@@ -11,7 +11,6 @@ J = 4
 Q = C // 2
 BANK = 512
 LIST = 16
-LINE = 4
 QUADRANT = 32
 ROWS = 4
 F32 = mybir.dt.float32
@@ -26,9 +25,11 @@ FP4X4 = mybir.dt.float4_e2m1fn_x4
 ACT = mybir.ActivationFunctionType
 ALU = mybir.AluOpType
 
-CHUNKS = ((0, 256, 256), (256, 256, 160), (512, 128, 88))
+CHUNKS = ((0, 256), (256, 256), (512, 128))
+ROW0_ON_VECTOR = 400
+RUN_ON = 8
 TURNED = 512
-PIECES = ((0, 128), (512, 128), (128, 128), (256, 256))
+PIECES = ((0, 128), (128, 256), (384, 256))
 
 
 def tile_moe_res_lin_relu2_kernel(tc, xT, xr, w_words, w_scales, b, gate, offs, out):
@@ -39,10 +40,13 @@ def tile_moe_res_lin_relu2_kernel(tc, xT, xr, w_words, w_scales, b, gate, offs, 
         psum = ctx.enter_context(tc.psum_pool(name="psum", bufs=1))
 
         offsets = keep.tile([P, E * C // LIST], U16, name="offsets")
-        raws = [keep.tile([P, J, n], F32, name=f"raw{t0}") for t0, n, on_vector in CHUNKS]
-        rounded = [keep.tile([P, n, J], BF16, align_bytes=64, name=f"rounded{t0}") for t0, n, on_vector in CHUNKS]
-        codes = keep.tile([P, T], U32, align_bytes=64, name="codes")
-        scales = keep.tile([P, T], U8, align_bytes=64, name="scales")
+        rows = [keep.tile([P, T], F32, name=f"row{j}") for j in range(2)]
+        planes = keep.tile([P, 2 * T], BF16, name="planes")
+        raws = [keep.tile([P, 2, n], F32, name=f"raw{t0}") for t0, n in CHUNKS]
+        table = keep.tile([P, 2 * T + J * Q], BF16, align_bytes=64, name="table")
+        second_values = keep.tile([P, J * Q], BF16, align_bytes=64, name="second_values")
+        last_values = keep.tile([P, J * C], BF16, align_bytes=64, name="last_values")
+        values = (table[:, 2 * T : 2 * T + J * Q], second_values[:], last_values[:, 0 : J * Q], last_values[:, J * Q : J * C])
         w_codes = keep.tile([P, E, 2 * N], U8, align_bytes=64, name="w_codes")
         w_scale = keep.tile([P, E, N], U8, align_bytes=64, name="w_scale")
         bias = keep.tile([P, E], F32, name="bias")
@@ -53,15 +57,16 @@ def tile_moe_res_lin_relu2_kernel(tc, xT, xr, w_words, w_scales, b, gate, offs, 
         identity = keep.tile([P, P], F32, name="identity")
         banks = [psum.tile([N, BANK], F32, name=f"bank{i}") for i in range(E * C // Q)]
 
-        nc.vector.memset(scales[:].bitcast(I32), 0)
         nc.vector.memset(main[:], 0.0)
         nc.vector.memset(side[:], 0.0)
         make_identity(nc, identity[:])
 
         x_rows = xT.rearrange("(p j) t -> p j t", j=J)
-        for raw, (t0, n, on_vector) in zip(raws, CHUNKS):
-            nc.sync.dma_start(out=raw[:], in_=x_rows[:, :, t0 : t0 + n])
+        nc.sync.dma_start(out=rows[0][:], in_=x_rows[:, 0, :])
         nc.sync.dma_start(offsets[:], offs)
+        nc.sync.dma_start(out=rows[1][:], in_=x_rows[:, 1, :])
+        for raw, (t0, n) in zip(raws, CHUNKS):
+            nc.sync.dma_start(out=raw[:], in_=x_rows[:, 2:J, t0 : t0 + n])
         nc.sync.dma_start(out=w_codes[:].bitcast(I32), in_=w_words.rearrange("e a p c -> p (e a) c").bitcast(I32))
         for r in range(ROWS):
             nc.sync.dma_start(
@@ -69,29 +74,42 @@ def tile_moe_res_lin_relu2_kernel(tc, xT, xr, w_words, w_scales, b, gate, offs, 
                 in_=w_scales.rearrange("e a (g r) n -> r g (e a) n", r=ROWS)[r].bitcast(I32),
             )
         nc.sync.dma_start(out=gates[:], in_=gate)
-        nc.sync.dma_start(out=bias[:], in_=b)
+        nc.gpsimd.dma_start(out=bias[:], in_=b)
         nc.sync.dma_start(out=resid[:], in_=xr)
-
-        for raw, tokens, (t0, n, on_vector) in zip(raws, rounded, CHUNKS):
-            src = raw[:].rearrange("p j (c i) -> p c j i", i=LINE)
-            dst = tokens[:].rearrange("p (c i) j -> p c j i", i=LINE)
-            cut = on_vector // LINE
-            nc.vector.tensor_copy(dst[:, 0:cut], src[:, 0:cut])
-            if on_vector < n:
-                nc.scalar.activation(dst[:, cut : n // LINE], src[:, cut : n // LINE], ACT.Copy)
-            nc.vector.quantize_mx(
-                out=codes[:, t0 : t0 + n].bitcast(FP8X4),
-                scales=scales[:, t0 : t0 + n],
-                in_=tokens[:].rearrange("p t j -> p (t j)"),
-            )
 
         def entries(s0, n):
             return offsets[:, s0 // LIST : (s0 + n) // LIST]
 
-        def gather(table, dtype, s0, n, name):
-            got = keep.tile([P, n], dtype, align_bytes=64, name=name)
-            nc.vector.tensor_copy(got[:], table[:].indirect(entries(s0, n)))
-            return got
+        def place(quarter, j):
+            return values[quarter].rearrange("p (s j) -> p s j", j=J)[:, :, j]
+
+        def gather_row(quarter, j, columns):
+            window = planes[:, j * T : j * T + columns]
+            nc.scalar.activation(place(quarter, j), window.indirect(entries(quarter * Q, Q)), ACT.Copy)
+
+        nc.scalar.activation(planes[:, ROW0_ON_VECTOR:T], rows[0][:, ROW0_ON_VECTOR:T], ACT.Copy)
+        nc.vector.tensor_copy(planes[:, 0:ROW0_ON_VECTOR], rows[0][:, 0:ROW0_ON_VECTOR])
+        nc.vector.tensor_copy(place(3, 0), rows[0][:].indirect(entries(3 * Q, Q)))
+        nc.vector.tensor_copy(planes[:, T : 2 * T], rows[1][:])
+        nc.vector.tensor_copy(place(3, 1), rows[1][:].indirect(entries(3 * Q, Q)))
+        for j in range(2):
+            for quarter in range(2):
+                gather_row(quarter, j, T)
+        gather_row(2, 0, T + 2 * RUN_ON)
+        gather_row(2, 1, T)
+        pairs = table[:, 0 : 2 * T].rearrange("p (t j) -> p t j", j=2)
+        for raw, (t0, n) in zip(raws, CHUNKS):
+            nc.vector.tensor_copy(pairs[:, t0 : t0 + n, :], raw[:].rearrange("p j t -> p t j"))
+
+        def gather_pairs(dst, s0, n, words):
+            window = table[:, 0 : 2 * words].bitcast(U32)
+            nc.vector.tensor_copy(dst.bitcast(U32).rearrange("p (s h) -> p s h", h=2)[:, :, 1], window.indirect(entries(s0, n)))
+
+        def quantise(src, n, name):
+            slot_codes = keep.tile([P, n], U32, align_bytes=64, name=f"{name}_codes")
+            slot_scales = keep.tile([P, n], U8, align_bytes=64, name=f"{name}_scales")
+            nc.vector.quantize_mx(out=slot_codes[:].bitcast(FP8X4), scales=slot_scales[:], in_=src)
+            return slot_codes, slot_scales
 
         def product(e, acc, slot_codes, slot_scales):
             nc.tensor.matmul_mx(
@@ -104,14 +122,14 @@ def tile_moe_res_lin_relu2_kernel(tc, xT, xr, w_words, w_scales, b, gate, offs, 
                 stop=True,
             )
 
-        def relu2(e, sums, name):
+        def relu2(e, sums, name, tag):
             width = sums[0].shape[1]
-            relus = [scratch.tile([N, width], F32, name=f"relu_{name}{i}", tag=f"scratch{i}") for i in range(2)]
-            square = keep.tile([N, 2 * width], F32, name=f"square_{name}")
-            for relu, acc in zip(relus, sums):
-                nc.scalar.activation(relu[:], acc, ACT.Relu, bias=bias[:, e : e + 1])
-            for i, relu in enumerate(relus):
-                nc.scalar.activation(square[:, i * width : (i + 1) * width], relu[:], ACT.Square)
+            relu = scratch.tile([N, len(sums), width], F32, name=f"relu_{name}", tag=tag)
+            square = keep.tile([N, len(sums) * width], F32, name=f"square_{name}")
+            for i, acc in enumerate(sums):
+                nc.scalar.activation(relu[:, i, :], acc, ACT.Relu, bias=bias[:, e : e + 1])
+            for i in range(len(sums)):
+                nc.scalar.activation(square[:, i * width : (i + 1) * width], relu[:, i, :], ACT.Square)
             return square
 
         def scatter(window, s0, n, square):
@@ -120,40 +138,45 @@ def tile_moe_res_lin_relu2_kernel(tc, xT, xr, w_words, w_scales, b, gate, offs, 
         def turn(dst, src, start, stop):
             nc.tensor.matmul(dst, src, identity[:], start=start, stop=stop, is_transpose=True)
 
-        first_scales = gather(scales, U8, 0, Q, "first_scales")
-        product(0, banks[0][:, 0:Q], gather(codes, U32, 0, Q, "first_codes")[:], first_scales[:])
-        first = relu2(0, (banks[0][:, 0 : Q // 2], banks[0][:, Q // 2 : Q]), "first")
-        second_scales = gather(scales, U8, Q, Q, "second_scales")
-        product(0, banks[1][:, 0:Q], gather(codes, U32, Q, Q, "second_codes")[:], second_scales[:])
-        second = relu2(0, (banks[1][:, 0 : Q // 2], banks[1][:, Q // 2 : Q]), "second")
-        last_scales = gather(scales, U8, C, C, "slot_scales23")
-        last_codes = gather(codes, U32, C, C, "last_codes")
-        product(1, banks[2][:, 0:Q], last_codes[:, 0:Q], last_scales[:, 0:Q])
-        product(1, banks[3][:, 0:Q], last_codes[:, Q:C], last_scales[:, Q:C])
-        last = relu2(1, (banks[2][:, 0:Q], banks[3][:, 0:Q]), "last")
+        gather_pairs(values[0], 0, Q, T)
+        gather_pairs(values[1], Q, Q, T)
+        first_codes, first_scales = quantise(values[0], Q, "first")
+        product(0, banks[0][:, 0:Q], first_codes[:], first_scales[:])
+        first = relu2(0, (banks[0][:, 0 : Q // 2], banks[0][:, Q // 2 : Q]), "first", "alone")
+        second_codes, second_scales = quantise(values[1], Q, "second")
+        product(0, banks[1][:, 0:Q], second_codes[:], second_scales[:])
+        second = relu2(0, (banks[1][:, 0:Q],), "second", "shared")
+        for quarter in (2, 3):
+            gather_pairs(values[quarter], quarter * Q, Q, T + RUN_ON)
+        for quarter in (2, 3):
+            slot_codes, slot_scales = quantise(values[quarter], Q, f"last{quarter}")
+            product(1, banks[quarter][:, 0:Q], slot_codes[:], slot_scales[:])
+        last = relu2(1, (banks[2][:, 0:Q], banks[3][:, 0:Q]), "last", "shared")
 
-        for i, bank in enumerate(banks):
+        sums = [psum.tile([P, BANK], F32, name=f"sum{i}") for i in range(TURNED // P)]
+        for i, bank in enumerate(sums):
             turn(bank[:, 0:P], resid[:, i * P : (i + 1) * P], True, False)
         scatter(main, 0, Q, first)
         scatter(side, Q, Q, second)
         scatter(main, C, C, last)
-        flipped = scratch.tile([P, TURNED], F32, name="flipped", tag="scratch1")
-        for i, bank in enumerate(banks):
+        flipped = scratch.tile([P, TURNED], F32, name="flipped", tag="shared")
+        for i, bank in enumerate(sums):
             turn(bank[:, 0:P], side[:, i * P : (i + 1) * P], False, True)
             nc.scalar.copy(flipped[:, i * P : (i + 1) * P], bank[:, 0:P])
         partial = {}
-        for t0, n in PIECES:
-            if t0 < TURNED:
-                partial[t0] = psum.tile([N, BANK], F32, name=f"partial{t0}")
-                for col in range(0, n, P):
-                    turn(partial[t0][:, col : col + P], flipped[:, t0 + col : t0 + col + P], True, True)
+        for bank, (t0, n) in zip(banks, PIECES):
+            partial[t0] = bank
+            for col in range(t0, min(t0 + n, TURNED), P):
+                turn(partial[t0][:, col - t0 : col - t0 + P], flipped[:, col : col + P], True, True)
 
-        partial[TURNED] = keep.tile([N, T - TURNED], F32, name="partial_sbuf")
-        nc.vector.tensor_tensor(partial[TURNED][:], resid[:, TURNED:T], side[:, TURNED:T], ALU.add)
+        rest = keep.tile([N, T - TURNED], F32, name="rest")
+        nc.vector.tensor_tensor(rest[:], resid[:, TURNED:T], side[:, TURNED:T], ALU.add)
 
-        for t0, n in PIECES:
+        for i, (t0, n) in enumerate(PIECES):
             result = keep.tile([N, n], F32, name=f"result{t0}")
-            engine = nc.vector if t0 < TURNED else nc.gpsimd
-            engine.tensor_tensor(result[:], partial[t0][:, 0:n], main[:, t0 : t0 + n], ALU.add)
-            queue = nc.sync if t0 < TURNED else nc.scalar
+            m = min(t0 + n, TURNED) - t0
+            if m < n:
+                nc.gpsimd.tensor_tensor(result[:, m:n], rest[:], main[:, TURNED:T], ALU.add)
+            nc.vector.tensor_tensor(result[:, 0:m], partial[t0][:, 0:m], main[:, t0 : t0 + m], ALU.add)
+            queue = nc.sync if i % 2 else nc.scalar
             queue.dma_start(out=out[:, t0 : t0 + n], in_=result[:])

@@ -29,7 +29,7 @@ CHUNKS = ((0, 256), (256, 256), (512, 128))
 ROW0_ON_VECTOR = 400
 RUN_ON = 8
 TURNED = 512
-PIECES = ((0, 128), (128, 256), (384, 256))
+PIECES = ((0, 128), (512, 128), (128, 128), (256, 256))
 
 
 def tile_moe_res_lin_relu2_kernel(tc, xT, xr, w_words, w_scales, b, gate, offs, out):
@@ -57,8 +57,9 @@ def tile_moe_res_lin_relu2_kernel(tc, xT, xr, w_words, w_scales, b, gate, offs, 
         identity = keep.tile([P, P], F32, name="identity")
         banks = [psum.tile([N, BANK], F32, name=f"bank{i}") for i in range(E * C // Q)]
 
-        nc.vector.memset(main[:], 0.0)
-        nc.vector.memset(side[:], 0.0)
+        for window in (main, side):
+            nc.vector.memset(window[:, 0 : T // 2 + 1], 0.0)
+            nc.vector.memset(window[:, T // 2 + 1 : T], 0.0)
         make_identity(nc, identity[:])
 
         x_rows = xT.rearrange("(p j) t -> p j t", j=J)
@@ -69,7 +70,8 @@ def tile_moe_res_lin_relu2_kernel(tc, xT, xr, w_words, w_scales, b, gate, offs, 
             nc.sync.dma_start(out=raw[:], in_=x_rows[:, 2:J, t0 : t0 + n])
         nc.sync.dma_start(out=w_codes[:].bitcast(I32), in_=w_words.rearrange("e a p c -> p (e a) c").bitcast(I32))
         for r in range(ROWS):
-            nc.sync.dma_start(
+            queue = nc.scalar if r == 0 else nc.sync
+            queue.dma_start(
                 out=w_scale[r:P:QUADRANT, :, :].bitcast(I32),
                 in_=w_scales.rearrange("e a (g r) n -> r g (e a) n", r=ROWS)[r].bitcast(I32),
             )
@@ -164,19 +166,17 @@ def tile_moe_res_lin_relu2_kernel(tc, xT, xr, w_words, w_scales, b, gate, offs, 
             turn(bank[:, 0:P], side[:, i * P : (i + 1) * P], False, True)
             nc.scalar.copy(flipped[:, i * P : (i + 1) * P], bank[:, 0:P])
         partial = {}
-        for bank, (t0, n) in zip(banks, PIECES):
+        for bank, (t0, n) in zip(banks, [piece for piece in PIECES if piece[0] < TURNED]):
             partial[t0] = bank
-            for col in range(t0, min(t0 + n, TURNED), P):
-                turn(partial[t0][:, col - t0 : col - t0 + P], flipped[:, col : col + P], True, True)
+            for col in range(0, n, P):
+                turn(bank[:, col : col + P], flipped[:, t0 + col : t0 + col + P], True, True)
 
-        rest = keep.tile([N, T - TURNED], F32, name="rest")
-        nc.vector.tensor_tensor(rest[:], resid[:, TURNED:T], side[:, TURNED:T], ALU.add)
+        partial[TURNED] = keep.tile([N, T - TURNED], F32, name="partial_sbuf")
+        nc.vector.tensor_tensor(partial[TURNED][:], resid[:, TURNED:T], side[:, TURNED:T], ALU.add)
 
         for i, (t0, n) in enumerate(PIECES):
             result = keep.tile([N, n], F32, name=f"result{t0}")
-            m = min(t0 + n, TURNED) - t0
-            if m < n:
-                nc.gpsimd.tensor_tensor(result[:, m:n], rest[:], main[:, TURNED:T], ALU.add)
-            nc.vector.tensor_tensor(result[:, 0:m], partial[t0][:, 0:m], main[:, t0 : t0 + m], ALU.add)
-            queue = nc.sync if i % 2 else nc.scalar
+            engine = nc.vector if t0 < TURNED else nc.gpsimd
+            engine.tensor_tensor(result[:], partial[t0][:, 0:n], main[:, t0 : t0 + n], ALU.add)
+            queue = nc.scalar if i % 2 else nc.sync
             queue.dma_start(out=out[:, t0 : t0 + n], in_=result[:])

@@ -25,11 +25,11 @@ FP4X4 = mybir.dt.float4_e2m1fn_x4
 ACT = mybir.ActivationFunctionType
 ALU = mybir.AluOpType
 
-CHUNKS = ((0, 256), (256, 256), (512, 128))
+CHUNKS = ((0, 256), (256, 384))
 ROW0_ON_VECTOR = 400
 RUN_ON = 8
 TURNED = 512
-PIECES = ((0, 128), (512, 128), (128, 128), (256, 256))
+PIECES = ((0, 256), (256, 384))
 
 
 def tile_moe_res_lin_relu2_kernel(tc, xT, xr, w_words, w_scales, b, gate, offs, out):
@@ -42,11 +42,11 @@ def tile_moe_res_lin_relu2_kernel(tc, xT, xr, w_words, w_scales, b, gate, offs, 
         offsets = keep.tile([P, E * C // LIST], U16, name="offsets")
         rows = [keep.tile([P, T], F32, name=f"row{j}") for j in range(2)]
         planes = keep.tile([P, 2 * T], BF16, name="planes")
-        raws = [keep.tile([P, 2, n], F32, name=f"raw{t0}") for t0, n in CHUNKS]
+        late = keep.tile([P, 2, T], F32, name="late")
         table = keep.tile([P, 2 * T + J * Q], BF16, align_bytes=64, name="table")
-        second_values = keep.tile([P, J * Q], BF16, align_bytes=64, name="second_values")
+        first_values = keep.tile([P, J * Q], BF16, align_bytes=64, name="first_values")
         last_values = keep.tile([P, J * C], BF16, align_bytes=64, name="last_values")
-        values = (table[:, 2 * T : 2 * T + J * Q], second_values[:], last_values[:, 0 : J * Q], last_values[:, J * Q : J * C])
+        values = (first_values[:], table[:, 2 * T : 2 * T + J * Q], last_values[:, 0 : J * Q], last_values[:, J * Q : J * C])
         w_codes = keep.tile([P, E, 2 * N], U8, align_bytes=64, name="w_codes")
         w_scale = keep.tile([P, E, N], U8, align_bytes=64, name="w_scale")
         bias = keep.tile([P, E], F32, name="bias")
@@ -57,26 +57,25 @@ def tile_moe_res_lin_relu2_kernel(tc, xT, xr, w_words, w_scales, b, gate, offs, 
         identity = keep.tile([P, P], F32, name="identity")
         banks = [psum.tile([N, BANK], F32, name=f"bank{i}") for i in range(E * C // Q)]
 
-        for window in (main, side):
-            nc.vector.memset(window[:, 0 : T // 2 + 1], 0.0)
-            nc.vector.memset(window[:, T // 2 + 1 : T], 0.0)
+        nc.vector.memset(main[:], 0.0)
+        nc.vector.memset(side[:], 0.0)
         make_identity(nc, identity[:])
 
         x_rows = xT.rearrange("(p j) t -> p j t", j=J)
         nc.sync.dma_start(out=rows[0][:], in_=x_rows[:, 0, :])
         nc.sync.dma_start(offsets[:], offs)
+        nc.sync.dma_start(out=late[:, 0, :], in_=x_rows[:, 2, :])
         nc.sync.dma_start(out=rows[1][:], in_=x_rows[:, 1, :])
-        for raw, (t0, n) in zip(raws, CHUNKS):
-            nc.sync.dma_start(out=raw[:], in_=x_rows[:, 2:J, t0 : t0 + n])
+        for t0, n in CHUNKS:
+            nc.sync.dma_start(out=late[:, 1, t0 : t0 + n], in_=x_rows[:, 3, t0 : t0 + n])
         nc.sync.dma_start(out=w_codes[:].bitcast(I32), in_=w_words.rearrange("e a p c -> p (e a) c").bitcast(I32))
         for r in range(ROWS):
-            queue = nc.scalar if r == 0 else nc.sync
-            queue.dma_start(
+            nc.sync.dma_start(
                 out=w_scale[r:P:QUADRANT, :, :].bitcast(I32),
                 in_=w_scales.rearrange("e a (g r) n -> r g (e a) n", r=ROWS)[r].bitcast(I32),
             )
         nc.sync.dma_start(out=gates[:], in_=gate)
-        nc.gpsimd.dma_start(out=bias[:], in_=b)
+        nc.sync.dma_start(out=bias[:], in_=b)
         nc.sync.dma_start(out=resid[:], in_=xr)
 
         def entries(s0, n):
@@ -92,16 +91,19 @@ def tile_moe_res_lin_relu2_kernel(tc, xT, xr, w_words, w_scales, b, gate, offs, 
         nc.scalar.activation(planes[:, ROW0_ON_VECTOR:T], rows[0][:, ROW0_ON_VECTOR:T], ACT.Copy)
         nc.vector.tensor_copy(planes[:, 0:ROW0_ON_VECTOR], rows[0][:, 0:ROW0_ON_VECTOR])
         nc.vector.tensor_copy(place(3, 0), rows[0][:].indirect(entries(3 * Q, Q)))
+        nc.vector.tensor_copy(place(0, 2), late[:, 0, :].indirect(entries(0, Q)))
         nc.vector.tensor_copy(planes[:, T : 2 * T], rows[1][:])
-        nc.vector.tensor_copy(place(3, 1), rows[1][:].indirect(entries(3 * Q, Q)))
         for j in range(2):
-            for quarter in range(2):
+            for quarter in range(3 + j):
                 gather_row(quarter, j, T)
-        gather_row(2, 0, T + 2 * RUN_ON)
-        gather_row(2, 1, T)
         pairs = table[:, 0 : 2 * T].rearrange("p (t j) -> p t j", j=2)
-        for raw, (t0, n) in zip(raws, CHUNKS):
-            nc.vector.tensor_copy(pairs[:, t0 : t0 + n, :], raw[:].rearrange("p j t -> p t j"))
+
+        def round_pairs(t0, n):
+            nc.vector.tensor_copy(pairs[:, t0 : t0 + n, :], late[:, :, t0 : t0 + n].rearrange("p j t -> p t j"))
+
+        round_pairs(*CHUNKS[0])
+        nc.vector.tensor_copy(place(0, 3), late[:, 1, :].indirect(entries(0, Q)))
+        round_pairs(*CHUNKS[1])
 
         def gather_pairs(dst, s0, n, words):
             window = table[:, 0 : 2 * words].bitcast(U32)
@@ -124,9 +126,9 @@ def tile_moe_res_lin_relu2_kernel(tc, xT, xr, w_words, w_scales, b, gate, offs, 
                 stop=True,
             )
 
-        def relu2(e, sums, name, tag):
+        def relu2(e, sums, name):
             width = sums[0].shape[1]
-            relu = scratch.tile([N, len(sums), width], F32, name=f"relu_{name}", tag=tag)
+            relu = scratch.tile([N, len(sums), width], F32, name=f"relu_{name}", tag="shared")
             square = keep.tile([N, len(sums) * width], F32, name=f"square_{name}")
             for i, acc in enumerate(sums):
                 nc.scalar.activation(relu[:, i, :], acc, ACT.Relu, bias=bias[:, e : e + 1])
@@ -140,20 +142,19 @@ def tile_moe_res_lin_relu2_kernel(tc, xT, xr, w_words, w_scales, b, gate, offs, 
         def turn(dst, src, start, stop):
             nc.tensor.matmul(dst, src, identity[:], start=start, stop=stop, is_transpose=True)
 
-        gather_pairs(values[0], 0, Q, T)
-        gather_pairs(values[1], Q, Q, T)
         first_codes, first_scales = quantise(values[0], Q, "first")
         product(0, banks[0][:, 0:Q], first_codes[:], first_scales[:])
-        first = relu2(0, (banks[0][:, 0 : Q // 2], banks[0][:, Q // 2 : Q]), "first", "alone")
+        gather_pairs(values[1], Q, Q, T)
+        gather_pairs(values[2], 2 * Q, Q, T)
+        first = relu2(0, (banks[0][:, 0 : Q // 2], banks[0][:, Q // 2 : Q]), "first")
         second_codes, second_scales = quantise(values[1], Q, "second")
         product(0, banks[1][:, 0:Q], second_codes[:], second_scales[:])
-        second = relu2(0, (banks[1][:, 0:Q],), "second", "shared")
-        for quarter in (2, 3):
-            gather_pairs(values[quarter], quarter * Q, Q, T + RUN_ON)
+        second = relu2(0, (banks[1][:, 0 : Q // 2], banks[1][:, Q // 2 : Q]), "second")
+        gather_pairs(values[3], 3 * Q, Q, T + RUN_ON)
         for quarter in (2, 3):
             slot_codes, slot_scales = quantise(values[quarter], Q, f"last{quarter}")
             product(1, banks[quarter][:, 0:Q], slot_codes[:], slot_scales[:])
-        last = relu2(1, (banks[2][:, 0:Q], banks[3][:, 0:Q]), "last", "shared")
+        last = relu2(1, (banks[2][:, 0:Q], banks[3][:, 0:Q]), "last")
 
         sums = [psum.tile([P, BANK], F32, name=f"sum{i}") for i in range(TURNED // P)]
         for i, bank in enumerate(sums):
@@ -165,18 +166,17 @@ def tile_moe_res_lin_relu2_kernel(tc, xT, xr, w_words, w_scales, b, gate, offs, 
         for i, bank in enumerate(sums):
             turn(bank[:, 0:P], side[:, i * P : (i + 1) * P], False, True)
             nc.scalar.copy(flipped[:, i * P : (i + 1) * P], bank[:, 0:P])
-        partial = {}
-        for bank, (t0, n) in zip(banks, [piece for piece in PIECES if piece[0] < TURNED]):
-            partial[t0] = bank
-            for col in range(0, n, P):
-                turn(bank[:, col : col + P], flipped[:, t0 + col : t0 + col + P], True, True)
+        for bank, (t0, n) in zip(banks, PIECES):
+            for col in range(t0, min(t0 + n, TURNED), P):
+                turn(bank[:, col - t0 : col - t0 + P], flipped[:, col : col + P], True, True)
 
-        partial[TURNED] = keep.tile([N, T - TURNED], F32, name="partial_sbuf")
-        nc.vector.tensor_tensor(partial[TURNED][:], resid[:, TURNED:T], side[:, TURNED:T], ALU.add)
+        rest = keep.tile([N, T - TURNED], F32, name="rest")
+        nc.vector.tensor_tensor(rest[:], resid[:, TURNED:T], side[:, TURNED:T], ALU.add)
 
-        for i, (t0, n) in enumerate(PIECES):
+        for bank, (t0, n) in zip(banks, PIECES):
             result = keep.tile([N, n], F32, name=f"result{t0}")
-            engine = nc.vector if t0 < TURNED else nc.gpsimd
-            engine.tensor_tensor(result[:], partial[t0][:, 0:n], main[:, t0 : t0 + n], ALU.add)
-            queue = nc.scalar if i % 2 else nc.sync
-            queue.dma_start(out=out[:, t0 : t0 + n], in_=result[:])
+            m = min(t0 + n, TURNED) - t0
+            if m < n:
+                nc.gpsimd.tensor_tensor(result[:, m:n], rest[:], main[:, TURNED:T], ALU.add)
+            nc.vector.tensor_tensor(result[:, 0:m], bank[:, 0:m], main[:, t0 : t0 + m], ALU.add)
+            nc.scalar.dma_start(out=out[:, t0 : t0 + n], in_=result[:])

@@ -1,4 +1,5 @@
 from contextlib import ExitStack
+from itertools import accumulate
 
 import concourse.mybir as mybir
 from concourse.masks import make_identity
@@ -127,13 +128,14 @@ def tile_moe_res_lin_relu2_kernel(tc, xT, xr, w_words, w_scales, b, gate, offs, 
             )
 
         def relu2(e, sums, name):
-            width = sums[0].shape[1]
-            relu = scratch.tile([N, len(sums), width], F32, name=f"relu_{name}", tag="shared")
-            square = keep.tile([N, len(sums) * width], F32, name=f"square_{name}")
-            for i, acc in enumerate(sums):
-                nc.scalar.activation(relu[:, i, :], acc, ACT.Relu, bias=bias[:, e : e + 1])
-            for i in range(len(sums)):
-                nc.scalar.activation(square[:, i * width : (i + 1) * width], relu[:, i, :], ACT.Square)
+            ends = list(accumulate(acc.shape[1] for acc in sums))
+            parts = [slice(end - acc.shape[1], end) for end, acc in zip(ends, sums)]
+            relu = scratch.tile([N, ends[-1]], F32, name=f"relu_{name}", tag="shared")
+            square = keep.tile([N, ends[-1]], F32, name=f"square_{name}")
+            for part, acc in zip(parts, sums):
+                nc.scalar.activation(relu[:, part], acc, ACT.Relu, bias=bias[:, e : e + 1])
+            for part in parts:
+                nc.scalar.activation(square[:, part], relu[:, part], ACT.Square)
             return square
 
         def scatter(window, s0, n, square):
@@ -154,7 +156,7 @@ def tile_moe_res_lin_relu2_kernel(tc, xT, xr, w_words, w_scales, b, gate, offs, 
         for quarter in (2, 3):
             slot_codes, slot_scales = quantise(values[quarter], Q, f"last{quarter}")
             product(1, banks[quarter][:, 0:Q], slot_codes[:], slot_scales[:])
-        last = relu2(1, (banks[2][:, 0:Q], banks[3][:, 0:Q]), "last")
+        last = relu2(1, (banks[2][:, 0:Q], banks[3][:, 0 : Q // 2], banks[3][:, Q // 2 : Q]), "last")
 
         sums = [psum.tile([P, BANK], F32, name=f"sum{i}") for i in range(TURNED // P)]
         for i, bank in enumerate(sums):

@@ -1,8 +1,6 @@
 from contextlib import ExitStack
-from itertools import accumulate
 
 import concourse.mybir as mybir
-from concourse.masks import make_identity
 
 K, T, E, C, N = 512, 640, 2, 256, 128
 FLOPS = 2 * K * N * E * C
@@ -26,10 +24,8 @@ FP4X4 = mybir.dt.float4_e2m1fn_x4
 ACT = mybir.ActivationFunctionType
 ALU = mybir.AluOpType
 
-CHUNKS = ((0, 256), (256, 384))
-ROW0_ON_VECTOR = 400
-RUN_ON = 8
-TURNED = 512
+LAST_ROWS_ON_VECTOR = 3
+CLEARED_BY_SCALAR = 128
 PIECES = ((0, 256), (256, 384))
 
 
@@ -41,144 +37,105 @@ def tile_moe_res_lin_relu2_kernel(tc, xT, xr, w_words, w_scales, b, gate, offs, 
         psum = ctx.enter_context(tc.psum_pool(name="psum", bufs=1))
 
         offsets = keep.tile([P, E * C // LIST], U16, name="offsets")
-        rows = [keep.tile([P, T], F32, name=f"row{j}") for j in range(2)]
-        planes = keep.tile([P, 2 * T], BF16, name="planes")
-        late = keep.tile([P, 2, T], F32, name="late")
-        table = keep.tile([P, 2 * T + J * Q], BF16, align_bytes=64, name="table")
-        first_values = keep.tile([P, J * Q], BF16, align_bytes=64, name="first_values")
-        last_values = keep.tile([P, J * C], BF16, align_bytes=64, name="last_values")
-        values = (first_values[:], table[:, 2 * T : 2 * T + J * Q], last_values[:, 0 : J * Q], last_values[:, J * Q : J * C])
+        rows = [keep.tile([P, T], F32, name=f"row{j}") for j in range(J)]
+        planes = [None] + [keep.tile([P, J, Q], BF16, name=f"planes{q}") for q in range(1, 4)]
+        values = [keep.tile([P, J * Q], BF16, align_bytes=64, name=f"values{q}") for q in range(4)]
         w_codes = keep.tile([P, E, 2 * N], U8, align_bytes=64, name="w_codes")
         w_scale = keep.tile([P, E, N], U8, align_bytes=64, name="w_scale")
         bias = keep.tile([P, E], F32, name="bias")
         gates = keep.tile([P, E * C], F32, name="gates")
         resid = keep.tile([P, T], F32, name="resid")
-        main = keep.tile([P, T], F32, name="main")
-        side = keep.tile([P, T], F32, name="side")
-        identity = keep.tile([P, P], F32, name="identity")
-        banks = [psum.tile([N, BANK], F32, name=f"bank{i}") for i in range(E * C // Q)]
+        outer = keep.tile([P, T], F32, name="outer")
+        inner = keep.tile([P, T], F32, name="inner")
+        banks = [psum.tile([N, BANK], F32, name=f"bank{i}") for i in range(4)]
 
-        nc.vector.memset(main[:], 0.0)
-        nc.vector.memset(side[:], 0.0)
-        make_identity(nc, identity[:])
+        nc.vector.memset(outer[:], 0.0)
+        nc.vector.memset(inner[:, CLEARED_BY_SCALAR:T], 0.0)
+        nc.scalar.activation(inner[:, 0:CLEARED_BY_SCALAR], outer[:, 0:CLEARED_BY_SCALAR], ACT.Copy)
 
         x_rows = xT.rearrange("(p j) t -> p j t", j=J)
         nc.sync.dma_start(out=rows[0][:], in_=x_rows[:, 0, :])
         nc.sync.dma_start(offsets[:], offs)
-        nc.sync.dma_start(out=late[:, 0, :], in_=x_rows[:, 2, :])
-        nc.sync.dma_start(out=rows[1][:], in_=x_rows[:, 1, :])
-        for t0, n in CHUNKS:
-            nc.sync.dma_start(out=late[:, 1, t0 : t0 + n], in_=x_rows[:, 3, t0 : t0 + n])
+        for j in range(1, J):
+            nc.sync.dma_start(out=rows[j][:], in_=x_rows[:, j, :])
         nc.sync.dma_start(out=w_codes[:].bitcast(I32), in_=w_words.rearrange("e a p c -> p (e a) c").bitcast(I32))
         for r in range(ROWS):
             nc.sync.dma_start(
                 out=w_scale[r:P:QUADRANT, :, :].bitcast(I32),
                 in_=w_scales.rearrange("e a (g r) n -> r g (e a) n", r=ROWS)[r].bitcast(I32),
             )
-        nc.sync.dma_start(out=gates[:], in_=gate)
         nc.sync.dma_start(out=bias[:], in_=b)
+        nc.sync.dma_start(out=gates[:], in_=gate)
         nc.sync.dma_start(out=resid[:], in_=xr)
 
         def entries(s0, n):
             return offsets[:, s0 // LIST : (s0 + n) // LIST]
 
-        def place(quarter, j):
-            return values[quarter].rearrange("p (s j) -> p s j", j=J)[:, :, j]
+        first_places = values[0][:].rearrange("p (s j) -> p s j", j=J)
+        for j in range(J):
+            nc.vector.tensor_copy(first_places[:, :, j], rows[j][:].indirect(entries(0, Q)))
+            for q in range(1, 4):
+                picked = rows[j][:].indirect(entries(q * Q, Q))
+                if q == 3 and j < LAST_ROWS_ON_VECTOR:
+                    nc.vector.tensor_copy(planes[q][:, j, :], picked)
+                else:
+                    nc.scalar.activation(planes[q][:, j, :], picked, ACT.Copy)
 
-        def gather_row(quarter, j, columns):
-            window = planes[:, j * T : j * T + columns]
-            nc.scalar.activation(place(quarter, j), window.indirect(entries(quarter * Q, Q)), ACT.Copy)
+        def woven(q):
+            dst = values[q][:].rearrange("p (c i j) -> p c j i", i=4, j=J)
+            src = planes[q][:].rearrange("p j (c i) -> p c j i", i=4)
+            return dst, src
 
-        nc.scalar.activation(planes[:, ROW0_ON_VECTOR:T], rows[0][:, ROW0_ON_VECTOR:T], ACT.Copy)
-        nc.vector.tensor_copy(planes[:, 0:ROW0_ON_VECTOR], rows[0][:, 0:ROW0_ON_VECTOR])
-        nc.vector.tensor_copy(place(3, 0), rows[0][:].indirect(entries(3 * Q, Q)))
-        nc.vector.tensor_copy(place(0, 2), late[:, 0, :].indirect(entries(0, Q)))
-        nc.vector.tensor_copy(planes[:, T : 2 * T], rows[1][:])
-        for j in range(2):
-            for quarter in range(3 + j):
-                gather_row(quarter, j, T)
-        pairs = table[:, 0 : 2 * T].rearrange("p (t j) -> p t j", j=2)
-
-        def round_pairs(t0, n):
-            nc.vector.tensor_copy(pairs[:, t0 : t0 + n, :], late[:, :, t0 : t0 + n].rearrange("p j t -> p t j"))
-
-        round_pairs(*CHUNKS[0])
-        nc.vector.tensor_copy(place(0, 3), late[:, 1, :].indirect(entries(0, Q)))
-        round_pairs(*CHUNKS[1])
-
-        def gather_pairs(dst, s0, n, words):
-            window = table[:, 0 : 2 * words].bitcast(U32)
-            nc.vector.tensor_copy(dst.bitcast(U32).rearrange("p (s h) -> p s h", h=2)[:, :, 1], window.indirect(entries(s0, n)))
-
-        def quantise(src, n, name):
-            slot_codes = keep.tile([P, n], U32, align_bytes=64, name=f"{name}_codes")
-            slot_scales = keep.tile([P, n], U8, align_bytes=64, name=f"{name}_scales")
-            nc.vector.quantize_mx(out=slot_codes[:].bitcast(FP8X4), scales=slot_scales[:], in_=src)
-            return slot_codes, slot_scales
-
-        def product(e, acc, slot_codes, slot_scales):
+        def product(q):
+            codes = keep.tile([P, Q], U32, align_bytes=64, name=f"codes{q}")
+            scales = keep.tile([P, Q], U8, align_bytes=64, name=f"scales{q}")
+            nc.vector.quantize_mx(out=codes[:].bitcast(FP8X4), scales=scales[:], in_=values[q][:])
+            e = q * Q // C
             nc.tensor.matmul_mx(
-                out=acc,
+                out=banks[q][:, 0:Q],
                 lhsT=w_codes[:, e, :].bitcast(FP4X4),
                 lhsT_scale=w_scale[:, e, :],
-                rhs=slot_codes.bitcast(FP8X4),
-                rhs_scale=slot_scales,
+                rhs=codes[:].bitcast(FP8X4),
+                rhs_scale=scales[:],
                 start=True,
                 stop=True,
             )
 
-        def relu2(e, sums, name):
-            ends = list(accumulate(acc.shape[1] for acc in sums))
-            parts = [slice(end - acc.shape[1], end) for end, acc in zip(ends, sums)]
-            relu = scratch.tile([N, ends[-1]], F32, name=f"relu_{name}", tag="shared")
-            square = keep.tile([N, ends[-1]], F32, name=f"square_{name}")
-            for part, acc in zip(parts, sums):
-                nc.scalar.activation(relu[:, part], acc, ACT.Relu, bias=bias[:, e : e + 1])
-            for part in parts:
-                nc.scalar.activation(square[:, part], relu[:, part], ACT.Square)
-            return square
+        nc.scalar.copy(*woven(3))
+        nc.vector.tensor_copy(*woven(1))
+        product(0)
+        nc.vector.tensor_copy(*woven(2))
+        for q in range(1, 4):
+            product(q)
 
-        def scatter(window, s0, n, square):
-            nc.vector.tensor_tensor(window[:].indirect(entries(s0, n)), square[:], gates[:, s0 : s0 + n], ALU.mult)
+        squares = keep.tile([N, E * C], F32, name="squares")
 
-        def turn(dst, src, start, stop):
-            nc.tensor.matmul(dst, src, identity[:], start=start, stop=stop, is_transpose=True)
+        def relu2(parts, name):
+            s0, s1 = parts[0][0], parts[-1][0] + parts[-1][1]
+            relu = scratch.tile([N, s1 - s0], F32, name=f"relu_{name}", tag="relu")
+            for first, n in parts:
+                e = first // C
+                acc = banks[first // Q][:, first % Q : first % Q + n]
+                nc.scalar.activation(relu[:, first - s0 : first - s0 + n], acc, ACT.Relu, bias=bias[:, e : e + 1])
+            for first, n in parts:
+                nc.scalar.activation(squares[:, first : first + n], relu[:, first - s0 : first - s0 + n], ACT.Square)
 
-        first_codes, first_scales = quantise(values[0], Q, "first")
-        product(0, banks[0][:, 0:Q], first_codes[:], first_scales[:])
-        gather_pairs(values[1], Q, Q, T)
-        gather_pairs(values[2], 2 * Q, Q, T)
-        first = relu2(0, (banks[0][:, 0 : Q // 2], banks[0][:, Q // 2 : Q]), "first")
-        second_codes, second_scales = quantise(values[1], Q, "second")
-        product(0, banks[1][:, 0:Q], second_codes[:], second_scales[:])
-        second = relu2(0, (banks[1][:, 0 : Q // 2], banks[1][:, Q // 2 : Q]), "second")
-        gather_pairs(values[3], 3 * Q, Q, T + RUN_ON)
-        for quarter in (2, 3):
-            slot_codes, slot_scales = quantise(values[quarter], Q, f"last{quarter}")
-            product(1, banks[quarter][:, 0:Q], slot_codes[:], slot_scales[:])
-        last = relu2(1, (banks[2][:, 0:Q], banks[3][:, 0 : Q // 2], banks[3][:, Q // 2 : Q]), "last")
+        relu2(((0, Q // 2), (Q // 2, Q // 2)), "first")
+        relu2(((Q, Q), (2 * Q, Q), (3 * Q, Q)), "rest")
 
-        sums = [psum.tile([P, BANK], F32, name=f"sum{i}") for i in range(TURNED // P)]
-        for i, bank in enumerate(sums):
-            turn(bank[:, 0:P], resid[:, i * P : (i + 1) * P], True, False)
-        scatter(main, 0, Q, first)
-        scatter(side, Q, Q, second)
-        scatter(main, C, C, last)
-        flipped = scratch.tile([P, TURNED], F32, name="flipped", tag="shared")
-        for i, bank in enumerate(sums):
-            turn(bank[:, 0:P], side[:, i * P : (i + 1) * P], False, True)
-            nc.scalar.copy(flipped[:, i * P : (i + 1) * P], bank[:, 0:P])
-        for bank, (t0, n) in zip(banks, PIECES):
-            for col in range(t0, min(t0 + n, TURNED), P):
-                turn(bank[:, col - t0 : col - t0 + P], flipped[:, col : col + P], True, True)
+        def scatter(s0, n):
+            nc.vector.tensor_tensor(outer[:].indirect(entries(s0, n)), squares[:, s0 : s0 + n], gates[:, s0 : s0 + n], ALU.mult)
 
-        rest = keep.tile([N, T - TURNED], F32, name="rest")
-        nc.vector.tensor_tensor(rest[:], resid[:, TURNED:T], side[:, TURNED:T], ALU.add)
+        scatter(0, Q)
+        gated = keep.tile([N, 2 * Q], F32, name="gated")
+        nc.vector.tensor_tensor(gated[:], squares[:, Q : 3 * Q], gates[:, Q : 3 * Q], ALU.mult)
+        nc.scalar.activation(inner[:].indirect(entries(Q, 2 * Q)), gated[:], ACT.Copy)
+        scatter(3 * Q, Q)
 
-        for bank, (t0, n) in zip(banks, PIECES):
+        partial = [keep.tile([N, n], F32, name=f"partial{t0}") for t0, n in PIECES]
+        for tile, (t0, n) in zip(partial, PIECES):
+            nc.vector.tensor_tensor(tile[:], resid[:, t0 : t0 + n], outer[:, t0 : t0 + n], ALU.add)
+        for tile, (t0, n) in zip(partial, PIECES):
             result = keep.tile([N, n], F32, name=f"result{t0}")
-            m = min(t0 + n, TURNED) - t0
-            if m < n:
-                nc.gpsimd.tensor_tensor(result[:, m:n], rest[:], main[:, TURNED:T], ALU.add)
-            nc.vector.tensor_tensor(result[:, 0:m], bank[:, 0:m], main[:, t0 : t0 + m], ALU.add)
+            nc.vector.tensor_tensor(result[:], tile[:], inner[:, t0 : t0 + n], ALU.add)
             nc.scalar.dma_start(out=out[:, t0 : t0 + n], in_=result[:])

@@ -24,7 +24,6 @@ FP4X4 = mybir.dt.float4_e2m1fn_x4
 ACT = mybir.ActivationFunctionType
 ALU = mybir.AluOpType
 
-LAST_ROWS_ON_VECTOR = 3
 CLEARED_BY_SCALAR = 128
 PIECES = ((0, 256), (256, 384))
 
@@ -76,7 +75,7 @@ def tile_moe_res_lin_relu2_kernel(tc, xT, xr, w_words, w_scales, b, gate, offs, 
             nc.vector.tensor_copy(first_places[:, :, j], rows[j][:].indirect(entries(0, Q)))
             for q in range(1, 4):
                 picked = rows[j][:].indirect(entries(q * Q, Q))
-                if q == 3 and j < LAST_ROWS_ON_VECTOR:
+                if q == 1:
                     nc.vector.tensor_copy(planes[q][:, j, :], picked)
                 else:
                     nc.scalar.activation(planes[q][:, j, :], picked, ACT.Copy)
@@ -101,10 +100,10 @@ def tile_moe_res_lin_relu2_kernel(tc, xT, xr, w_words, w_scales, b, gate, offs, 
                 stop=True,
             )
 
-        nc.scalar.copy(*woven(3))
-        nc.vector.tensor_copy(*woven(1))
+        nc.scalar.copy(*woven(2))
         product(0)
-        nc.vector.tensor_copy(*woven(2))
+        nc.vector.tensor_copy(*woven(1))
+        nc.vector.tensor_copy(*woven(3))
         for q in range(1, 4):
             product(q)
 

@@ -24,6 +24,7 @@ FP4X4 = mybir.dt.float4_e2m1fn_x4
 ACT = mybir.ActivationFunctionType
 ALU = mybir.AluOpType
 
+EARLY_CUT = 256
 CLEARED_BY_SCALAR = 128
 PIECES = ((0, 256), (256, 384))
 
@@ -37,7 +38,7 @@ def tile_moe_res_lin_relu2_kernel(tc, xT, xr, w_words, w_scales, b, gate, offs, 
 
         offsets = keep.tile([P, E * C // LIST], U16, name="offsets")
         rows = [keep.tile([P, T], F32, name=f"row{j}") for j in range(J)]
-        planes = [None] + [keep.tile([P, J, Q], BF16, name=f"planes{q}") for q in range(1, 4)]
+        planes = keep.tile([P, J, 3 * Q], BF16, name="planes")
         values = [keep.tile([P, J * Q], BF16, align_bytes=64, name=f"values{q}") for q in range(4)]
         w_codes = keep.tile([P, E, 2 * N], U8, align_bytes=64, name="w_codes")
         w_scale = keep.tile([P, E, N], U8, align_bytes=64, name="w_scale")
@@ -73,16 +74,14 @@ def tile_moe_res_lin_relu2_kernel(tc, xT, xr, w_words, w_scales, b, gate, offs, 
         first_places = values[0][:].rearrange("p (s j) -> p s j", j=J)
         for j in range(J):
             nc.vector.tensor_copy(first_places[:, :, j], rows[j][:].indirect(entries(0, Q)))
-            for q in range(1, 4):
-                picked = rows[j][:].indirect(entries(q * Q, Q))
-                if q == 1:
-                    nc.vector.tensor_copy(planes[q][:, j, :], picked)
-                else:
-                    nc.scalar.activation(planes[q][:, j, :], picked, ACT.Copy)
+            cut = EARLY_CUT if j < J - 1 else C
+            nc.vector.tensor_copy(planes[:, j, 0 : cut - Q], rows[j][:].indirect(entries(Q, cut - Q)))
+            for s0, s1 in ((cut, E * C),) if j < J - 1 else ((C, C + Q), (C + Q, E * C)):
+                nc.scalar.activation(planes[:, j, s0 - Q : s1 - Q], rows[j][:].indirect(entries(s0, s1 - s0)), ACT.Copy)
 
         def woven(q):
             dst = values[q][:].rearrange("p (c i j) -> p c j i", i=4, j=J)
-            src = planes[q][:].rearrange("p j (c i) -> p c j i", i=4)
+            src = planes[:, :, (q - 1) * Q : q * Q].rearrange("p j (c i) -> p c j i", i=4)
             return dst, src
 
         def product(q):
@@ -127,7 +126,8 @@ def tile_moe_res_lin_relu2_kernel(tc, xT, xr, w_words, w_scales, b, gate, offs, 
 
         scatter(0, Q)
         gated = keep.tile([N, 2 * Q], F32, name="gated")
-        nc.vector.tensor_tensor(gated[:], squares[:, Q : 3 * Q], gates[:, Q : 3 * Q], ALU.mult)
+        for s0 in (Q, 2 * Q):
+            nc.vector.tensor_tensor(gated[:, s0 - Q : s0], squares[:, s0 : s0 + Q], gates[:, s0 : s0 + Q], ALU.mult)
         nc.scalar.activation(inner[:].indirect(entries(Q, 2 * Q)), gated[:], ACT.Copy)
         scatter(3 * Q, Q)
 

@@ -25,6 +25,7 @@ ACT = mybir.ActivationFunctionType
 ALU = mybir.AluOpType
 
 EARLY_CUT = 256
+LAST = 352
 CLEARED_BY_SCALAR = 128
 PIECES = ((0, 256), (256, 384))
 
@@ -108,28 +109,28 @@ def tile_moe_res_lin_relu2_kernel(tc, xT, xr, w_words, w_scales, b, gate, offs, 
 
         squares = keep.tile([N, E * C], F32, name="squares")
 
-        def relu2(parts, name):
+        def relu2(parts, name, cuts):
             s0, s1 = parts[0][0], parts[-1][0] + parts[-1][1]
             relu = scratch.tile([N, s1 - s0], F32, name=f"relu_{name}", tag="relu")
             for first, n in parts:
                 e = first // C
                 acc = banks[first // Q][:, first % Q : first % Q + n]
                 nc.scalar.activation(relu[:, first - s0 : first - s0 + n], acc, ACT.Relu, bias=bias[:, e : e + 1])
-            for first, n in parts:
-                nc.scalar.activation(squares[:, first : first + n], relu[:, first - s0 : first - s0 + n], ACT.Square)
+            for a, z in zip(cuts, cuts[1:]):
+                nc.scalar.activation(squares[:, a:z], relu[:, a - s0 : z - s0], ACT.Square)
 
-        relu2(((0, Q // 2), (Q // 2, Q // 2)), "first")
-        relu2(((Q, Q), (2 * Q, Q), (3 * Q, Q)), "rest")
+        relu2(((0, Q // 2), (Q // 2, Q // 2)), "first", (0, Q // 2, Q))
+        relu2(((Q, Q), (2 * Q, Q), (3 * Q, Q)), "rest", (Q, C, LAST, E * C))
 
         def scatter(s0, n):
             nc.vector.tensor_tensor(outer[:].indirect(entries(s0, n)), squares[:, s0 : s0 + n], gates[:, s0 : s0 + n], ALU.mult)
 
         scatter(0, Q)
-        gated = keep.tile([N, 2 * Q], F32, name="gated")
-        for s0 in (Q, 2 * Q):
-            nc.vector.tensor_tensor(gated[:, s0 - Q : s0], squares[:, s0 : s0 + Q], gates[:, s0 : s0 + Q], ALU.mult)
-        nc.scalar.activation(inner[:].indirect(entries(Q, 2 * Q)), gated[:], ACT.Copy)
-        scatter(3 * Q, Q)
+        gated = keep.tile([N, LAST - Q], F32, name="gated")
+        for s0, s1 in ((Q, C), (C, LAST)):
+            nc.vector.tensor_tensor(gated[:, s0 - Q : s1 - Q], squares[:, s0:s1], gates[:, s0:s1], ALU.mult)
+        nc.scalar.activation(inner[:].indirect(entries(Q, LAST - Q)), gated[:], ACT.Copy)
+        scatter(LAST, E * C - LAST)
 
         partial = [keep.tile([N, n], F32, name=f"partial{t0}") for t0, n in PIECES]
         for tile, (t0, n) in zip(partial, PIECES):

@@ -26,6 +26,7 @@ ALU = mybir.AluOpType
 
 EARLY_CUT = 256
 LAST = 352
+SHARE = 32
 CLEARED_BY_SCALAR = 128
 PIECES = ((0, 256), (256, 384))
 
@@ -80,9 +81,9 @@ def tile_moe_res_lin_relu2_kernel(tc, xT, xr, w_words, w_scales, b, gate, offs, 
             for s0, s1 in ((cut, E * C),) if j < J - 1 else ((C, C + Q), (C + Q, E * C)):
                 nc.scalar.activation(planes[:, j, s0 - Q : s1 - Q], rows[j][:].indirect(entries(s0, s1 - s0)), ACT.Copy)
 
-        def woven(q):
-            dst = values[q][:].rearrange("p (c i j) -> p c j i", i=4, j=J)
-            src = planes[:, :, (q - 1) * Q : q * Q].rearrange("p j (c i) -> p c j i", i=4)
+        def woven(q, s0=0, s1=Q):
+            dst = values[q][:, J * s0 : J * s1].rearrange("p (c i j) -> p c j i", i=4, j=J)
+            src = planes[:, :, (q - 1) * Q + s0 : (q - 1) * Q + s1].rearrange("p j (c i) -> p c j i", i=4)
             return dst, src
 
         def product(q):
@@ -101,9 +102,10 @@ def tile_moe_res_lin_relu2_kernel(tc, xT, xr, w_words, w_scales, b, gate, offs, 
             )
 
         nc.scalar.copy(*woven(2))
+        nc.scalar.copy(*woven(3, 0, SHARE))
         product(0)
         nc.vector.tensor_copy(*woven(1))
-        nc.vector.tensor_copy(*woven(3))
+        nc.vector.tensor_copy(*woven(3, SHARE, Q))
         for q in range(1, 4):
             product(q)
 

from contextlib import ExitStack

import concourse.mybir as mybir

K, T, E, C, N = 512, 640, 2, 256, 128
FLOPS = 2 * K * N * E * C

P = 128
J = 4
Q = C // 2
BANK = 512
LIST = 16
QUADRANT = 32
ROWS = 4
F32 = mybir.dt.float32
BF16 = mybir.dt.bfloat16
I32 = mybir.dt.int32
U32 = mybir.dt.uint32
U16 = mybir.dt.uint16
U8 = mybir.dt.uint8
FP8X4 = mybir.dt.float8_e4m3fn_x4
FP4X4 = mybir.dt.float4_e2m1fn_x4

ACT = mybir.ActivationFunctionType
ALU = mybir.AluOpType

EARLY_CUT = 256
LAST = 352
SHARE = 32
CLEARED_BY_SCALAR = 128
PIECES = ((0, 256), (256, 384))


def tile_moe_res_lin_relu2_kernel(tc, xT, xr, w_words, w_scales, b, gate, offs, out):
    nc = tc.nc
    with ExitStack() as ctx:
        keep = ctx.enter_context(tc.tile_pool(name="keep", bufs=1))
        scratch = ctx.enter_context(tc.tile_pool(name="scratch", bufs=1))
        psum = ctx.enter_context(tc.psum_pool(name="psum", bufs=1))

        offsets = keep.tile([P, E * C // LIST], U16, name="offsets")
        rows = [keep.tile([P, T], F32, name=f"row{j}") for j in range(J)]
        planes = keep.tile([P, J, 3 * Q], BF16, name="planes")
        values = [keep.tile([P, J * Q], BF16, align_bytes=64, name=f"values{q}") for q in range(4)]
        w_codes = keep.tile([P, E, 2 * N], U8, align_bytes=64, name="w_codes")
        w_scale = keep.tile([P, E, N], U8, align_bytes=64, name="w_scale")
        bias = keep.tile([P, E], F32, name="bias")
        gates = keep.tile([P, E * C], F32, name="gates")
        resid = keep.tile([P, T], F32, name="resid")
        outer = keep.tile([P, T], F32, name="outer")
        inner = keep.tile([P, T], F32, name="inner")
        banks = [psum.tile([N, BANK], F32, name=f"bank{i}") for i in range(4)]

        nc.vector.memset(outer[:], 0.0)
        nc.vector.memset(inner[:, CLEARED_BY_SCALAR:T], 0.0)
        nc.scalar.activation(inner[:, 0:CLEARED_BY_SCALAR], outer[:, 0:CLEARED_BY_SCALAR], ACT.Copy)

        x_rows = xT.rearrange("(p j) t -> p j t", j=J)
        nc.sync.dma_start(out=rows[0][:], in_=x_rows[:, 0, :])
        nc.sync.dma_start(offsets[:], offs)
        for j in range(1, J):
            nc.sync.dma_start(out=rows[j][:], in_=x_rows[:, j, :])
        nc.sync.dma_start(out=w_codes[:].bitcast(I32), in_=w_words.rearrange("e a p c -> p (e a) c").bitcast(I32))
        for r in range(ROWS):
            nc.sync.dma_start(
                out=w_scale[r:P:QUADRANT, :, :].bitcast(I32),
                in_=w_scales.rearrange("e a (g r) n -> r g (e a) n", r=ROWS)[r].bitcast(I32),
            )
        nc.sync.dma_start(out=bias[:], in_=b)
        nc.sync.dma_start(out=gates[:], in_=gate)
        nc.sync.dma_start(out=resid[:], in_=xr)

        def entries(s0, n):
            return offsets[:, s0 // LIST : (s0 + n) // LIST]

        first_places = values[0][:].rearrange("p (s j) -> p s j", j=J)
        for j in range(J):
            nc.vector.tensor_copy(first_places[:, :, j], rows[j][:].indirect(entries(0, Q)))
            cut = EARLY_CUT if j < J - 1 else C
            nc.vector.tensor_copy(planes[:, j, 0 : cut - Q], rows[j][:].indirect(entries(Q, cut - Q)))
            for s0, s1 in ((cut, E * C),) if j < J - 1 else ((C, C + Q), (C + Q, E * C)):
                nc.scalar.activation(planes[:, j, s0 - Q : s1 - Q], rows[j][:].indirect(entries(s0, s1 - s0)), ACT.Copy)

        def woven(q, s0=0, s1=Q):
            dst = values[q][:, J * s0 : J * s1].rearrange("p (c i j) -> p c j i", i=4, j=J)
            src = planes[:, :, (q - 1) * Q + s0 : (q - 1) * Q + s1].rearrange("p j (c i) -> p c j i", i=4)
            return dst, src

        def product(q):
            codes = keep.tile([P, Q], U32, align_bytes=64, name=f"codes{q}")
            scales = keep.tile([P, Q], U8, align_bytes=64, name=f"scales{q}")
            nc.vector.quantize_mx(out=codes[:].bitcast(FP8X4), scales=scales[:], in_=values[q][:])
            e = q * Q // C
            nc.tensor.matmul_mx(
                out=banks[q][:, 0:Q],
                lhsT=w_codes[:, e, :].bitcast(FP4X4),
                lhsT_scale=w_scale[:, e, :],
                rhs=codes[:].bitcast(FP8X4),
                rhs_scale=scales[:],
                start=True,
                stop=True,
            )

        nc.scalar.copy(*woven(2))
        nc.scalar.copy(*woven(3, 0, SHARE))
        product(0)
        nc.vector.tensor_copy(*woven(1))
        nc.vector.tensor_copy(*woven(3, SHARE, Q))
        for q in range(1, 4):
            product(q)

        squares = keep.tile([N, E * C], F32, name="squares")

        def relu2(parts, name, cuts):
            s0, s1 = parts[0][0], parts[-1][0] + parts[-1][1]
            relu = scratch.tile([N, s1 - s0], F32, name=f"relu_{name}", tag="relu")
            for first, n in parts:
                e = first // C
                acc = banks[first // Q][:, first % Q : first % Q + n]
                nc.scalar.activation(relu[:, first - s0 : first - s0 + n], acc, ACT.Relu, bias=bias[:, e : e + 1])
            for a, z in zip(cuts, cuts[1:]):
                nc.scalar.activation(squares[:, a:z], relu[:, a - s0 : z - s0], ACT.Square)

        relu2(((0, Q // 2), (Q // 2, Q // 2)), "first", (0, Q // 2, Q))
        relu2(((Q, Q), (2 * Q, Q), (3 * Q, Q)), "rest", (Q, C, LAST, E * C))

        def scatter(s0, n):
            nc.vector.tensor_tensor(outer[:].indirect(entries(s0, n)), squares[:, s0 : s0 + n], gates[:, s0 : s0 + n], ALU.mult)

        scatter(0, Q)
        gated = keep.tile([N, LAST - Q], F32, name="gated")
        for s0, s1 in ((Q, C), (C, LAST)):
            nc.vector.tensor_tensor(gated[:, s0 - Q : s1 - Q], squares[:, s0:s1], gates[:, s0:s1], ALU.mult)
        nc.scalar.activation(inner[:].indirect(entries(Q, LAST - Q)), gated[:], ACT.Copy)
        scatter(LAST, E * C - LAST)

        partial = [keep.tile([N, n], F32, name=f"partial{t0}") for t0, n in PIECES]
        for tile, (t0, n) in zip(partial, PIECES):
            nc.vector.tensor_tensor(tile[:], resid[:, t0 : t0 + n], outer[:, t0 : t0 + n], ALU.add)
        for tile, (t0, n) in zip(partial, PIECES):
            result = keep.tile([N, n], F32, name=f"result{t0}")
            nc.vector.tensor_tensor(result[:], tile[:], inner[:, t0 : t0 + n], ALU.add)
            nc.scalar.dma_start(out=out[:, t0 : t0 + n], in_=result[:])
